import numpy as np, ml_dtypes
CORES = [5,29,101,125,133,157,229,253]
N = 8
BF = ml_dtypes.bfloat16
P, U, S, RO, TH, PH = 2048, 128, 256, 3, 85, 85
def places(rng):
    c = rng.integers(0, 256, (N, 8, 3, 16)); c[:, :, 1] >>= 3
    k = rng.integers(0, 3, (N, 8, P)); a = rng.choice(np.array([4, 16, 48, 128, 255]), (N, 8, 1, P))
    m = np.take_along_axis(c, k[..., None], 2).transpose(0, 1, 3, 2)
    return np.clip(m + np.floor((2 * rng.random((N, 8, 16, P)) - 1) * a).astype(np.int64), 0, 255)
def near(rng, X, n):
    k = rng.integers(0, P, (N, 8, 1, n)); a = rng.choice(np.array([0, 8, 40, 160]), (N, 8, 1, n))
    return np.clip(np.take_along_axis(X, k, 3) + np.floor((2 * rng.random((N, 8, 16, n)) - 1) * a).astype(np.int64), 0, 255)
def parts(rng):
    X = places(rng); nb = rng.integers(0, P, (N, 8, 16, P)); v = rng.integers(0, P, (N, 8, U))
    A = np.where(rng.random((N, 8, 16, U)) < 0.6, v[:, :, None, :], rng.integers(0, P, (N, 8, 16, U)))
    return X, nb, v, A, near(rng, X, U), rng.integers(0, U, (N, 8, S)), near(rng, X, S), rng.integers(0, 4096, (N, 8, 16))
def pack(X, nb, v, A, y, j, z, w):
    fl = lambda a: np.ascontiguousarray(a.reshape(N, 128, -1)).astype(np.float32).astype(BF)
    wh = lambda a, p: np.ascontiguousarray(a.reshape(N, p, -1)).astype(np.int32)
    return {"x": fl(X), "nb": wh(nb, 128), "v0": wh(v, 8), "a0": wh(A, 128), "y0": fl(y), "j0": wh(j, 8), "z0": fl(z), "w": wh(w, 128)}
def setup_inputs(rng):
    return pack(*parts(rng))
def setup_inputs_spread(rng):
    def skew(hi, e, *shape): return (hi * rng.random(shape) ** e).astype(np.int64)
    def size(n): return np.minimum(np.exp2(8 * rng.random((N, 8, 1, n))) * rng.random((N, 8, 16, n)) * 1.5, 255).astype(np.int64)
    return pack(size(P), skew(P, 3, N, 8, 16, P), skew(P, 4, N, 8, U), skew(P, 2, N, 8, 16, U), size(U), skew(U, 3, N, 8, S), size(S), np.exp2(12 * rng.random((N, 8, 16))).astype(np.int64) - 1)
def setup_inputs_ends(rng):
    def edge(hi, *shape): return np.where(rng.random(shape) < 0.7, hi * rng.integers(0, 2, shape), rng.integers(0, hi + 1, shape))
    def bits(n):
        q = rng.integers(0, 4, (N, 8, 1, n)); m = rng.integers(0, 2, (N, 8, 16, n))
        return 255 * np.where(q == 0, 0, np.where(q == 1, 1, m))
    big = np.array([P - 1, P - 2, 1, 2, 3]); X = bits(P); X[:, :, :, 0] = 0; X[:, :, :, big] = 255
    nb = edge(P - 1, N, 8, 16, P); nb[:, 1::2, :, P - 1] = rng.choice(big, (N, 4, 16))
    v, A, y, j, z = edge(P - 1, N, 8, U), edge(P - 1, N, 8, 16, U), bits(U), edge(U - 1, N, 8, S), bits(S)
    for u in (0, 1, 6, U - 1):
        v[:, 1::2, u] = P - 1; y[:, 1::2, :, u] = 0; A[:, 1::2, 15, u] = 0; A[:, 1::2, 14, u] = P - 1
    w = 4095 * rng.integers(0, 2, (N, 8, 16)); w[:, 1] = 4095; w[:, 7] = 4095; w[:, 2] = 0
    for s in (0, S - 1): z[:, 7, :, s] = 255
    for s in (1, S - 2): z[:, 7, :, s] = 0; z[:, 7, 5, s] = 1; j[:, 7, s] = U - 1
    return pack(X, nb, v, A, y, j, z, w)
def level(s):
    return (s >> 4) + (np.arange(16) < (s & 15))
def setup_inputs_corners(rng):
    X, nb, v, A, y, j, z, w = parts(rng); kind = rng.permutation(8); a = np.arange(P); st = P // U; us = rng.permutation(U)
    ut = np.array([4075, 4087, 4089, 0, 0, 4095]); at = np.array([4093, 4089, 4087, 7, 100, 301]) & (P - 1)
    h = (((at * ut) >> 5) + at) & (P - 1); hw = (h + np.array([1, 1, 1, 128 * 7, 128 * 100, -128 * 301])) & (P - 1)
    zt = np.full((16, 6), 250); zt[0] = np.where(ut > 0, 251, 250); zt[14] = np.where(ut > 0, (ut - 3072) >> 4, 0); zt[15] = ut & 15
    for r in range(N):
        for g in range(8):
            f = kind[g]; Xg, n = X[r, g], nb[r, g]
            if f in (0, 4, 5):
                c = rng.integers(0, 256, (16, 1)); Xg[:] = c; y[r, g] = c; n[:] = (a ^ 1) if f == 5 else ((a + 1) & (P - 1))
                v[r, g] = st * rng.permutation(U) + st - 1; A[r, g] = v[r, g]; w[r, g] = rng.choice(np.array([0, 4095, 1, 2048]), 16) if f != 4 else 4095
            if f == 1: n[:] = a; A[r, g] = v[r, g]; w[r, g] = 0
            if f == 2:
                o = rng.permutation(P)
                for l in range(16):
                    for d in range(3): Xg[:, o[3 * l + d]] = level(TH * (l + 1) + d - 1); Xg[:, o[48 + 3 * l + d]] = level(PH * (l + 1) + d - 1)
                Xg[:, o[96]] = 0; Xg[:, o[97]] = level(8 * PH)
                v[r, g] = o[128:128 + U]; odd = np.arange(U) & 1; n[:, v[r, g]] = np.where(odd == 1, o[97], o[96])[None, :]
                y[r, g] = np.where(odd == 1, Xg[:, o[97]][:, None], 0)
                d = np.where(rng.random((16, U)) < 0.6 * odd, 2, rng.integers(0, 3, (16, U))); A[r, g] = o[3 * np.arange(16)[:, None] + d + 48 * odd]
                z[r, g] = 0
            if f == 3:
                q = rng.integers(0, 4, (16, P)); n[:] = np.where(q == 0, 0, np.where(q == 1, P - 1, np.where(q == 2, a, n)))
                q = rng.integers(0, 3, U); v[r, g] = np.where(q == 0, 0, np.where(q == 1, P - 1, v[r, g]))
                q = rng.integers(0, 3, (16, U)); A[r, g] = np.where(q == 0, 0, np.where(q == 1, P - 1, v[r, g])); j[r, g] = (U - 1) * rng.integers(0, 2, S)
            if f == 6: w[r, g] = 4095 * rng.integers(0, 2, 16)
            if f == 7:
                sp = np.concatenate([at, h, hw]); o = rng.permutation(np.setdiff1d(a, sp)); isp = np.zeros(P, bool); isp[sp] = True; isp[o[:8]] = True
                n[:] = np.where(isp[n], rng.choice(o[8:], (16, P)), n)
                v[r, g] = np.where(isp[v[r, g]], rng.choice(o[8:], U), v[r, g]); A[r, g] = np.where(isp[A[r, g]], rng.choice(o[8:], (16, U)), A[r, g])
                c = rng.integers(24, 57, (16, 1)); Xg[:, at] = c; Xg[:, h] = c; Xg[:, hw] = zt; Xg[:, o[:1]] = c; Xg[:, o[1:2]] = c + 60
                n[:, o[0]] = o[0]; v[r, g, us[:6]] = o[0]; y[r, g][:, us[:6]] = c; A[r, g][:15, us[:6]] = at; A[r, g][15, us[:6]] = o[1]
                Xg[:, o[4:8]] = np.stack([level(s) for s in (2052, 2051, 4080, 4079)], axis=1)
                n[:, o[2:4]] = o[[4, 6]]; n[15, o[2:4]] = o[[5, 7]]; v[r, g, us[6:8]] = o[2:4]; y[r, g][:, us[6:8]] = 0
                w[r, g] = 3072; w[r, g, 14] = 16; w[r, g, 15] = 1
                ss = rng.permutation(S)[:48].reshape(6, 8); z[r, g][:, ss] = zt[:, :, None]; j[r, g][ss] = us[:6][:, None]
    return pack(X, nb, v, A, y, j, z, w)
def setup_inputs_crowd(rng):
    X, nb, v, A, y, j, z, w = parts(rng); h = U // 2
    for q in range(N):
        home = (q - 1) % N; miss = int(rng.integers(0, 8))
        for g in range(8):
            Xg, n, m = X[q, g], nb[q, g], g & 3; pl = rng.permutation(P)
            if m == 2: i = int(np.argmin(pl)); pl[i] = pl[0]; pl[0] = 0
            o, e, b = pl[0], pl[1], pl[2]
            ev = pl[16:16 + h].copy() if m == 2 else np.full(h, e)
            if m & 1: ev[rng.integers(0, h)] = pl[3]
            od = np.full(h, o)
            if (g + q) & 1: od[rng.integers(0, h)] = pl[4]
            v[q, g, 0::2] = ev; v[q, g, 1::2] = od; n[:, ev] = ev[None, :]
            if m != 3: n[:, o] = b; n[:, pl[4]] = pl[5]
            Xg[:, b] = 10; Xg[:, o] = 250; Xg[:, pl[6]] = 240; Xg[:, e] = 200
            if m == 2: Xg[:, b] = 250; Xg[:, pl[8]] = 10; n[:, b] = pl[8]
            A[q, g, :, 0::2] = ev; A[q, g, :, 1::2] = (o, o, o, pl[6])[m]
            if m == 1: A[q, g, :, 1 + 2 * int(rng.integers(0, h))] = pl[6]
            t = 2 * rng.integers(0, h, S)
            if m == 0: t[:] = t[0]
            if m == 1: t[:] = t[0]; t[rng.integers(0, S)] = (t[0] + 2) % U
            if (q & 1) and g == miss:
                us = 2 * int(rng.integers(0, h)); Xg[:, pl[7]] = Xg[:, v[q, g, us]]; A[q, g, :, us] = pl[7]
                t = np.where(t == us, (us + 2) % U, t); t[rng.integers(0, S)] = us
            j[home, g] = t
    return pack(X, nb, v, A, y, j, z, w)
def setup_inputs_ties(rng):
    X, nb, v, A, y, j, z, w = parts(rng); c = 17 * rng.integers(0, 16, (N, 8, 16, 12)); c[:, 1::2, :, :6] = (c[:, 1::2, :, :6] >> 2) - ((c[:, 1::2, :, :6] >> 2) % 17)
    def some(n): return np.take_along_axis(c, rng.integers(0, 12, (N, 8, 1, n)), 3)
    X, y, z = some(P), some(U), some(S); nb[:, ::2, 8:] = nb[:, ::2, :8]; nb[:, 3, 1::2] = nb[:, 3, 0::2]
    v[:, 2] = rng.integers(0, 40, (N, U)); v[:, 5] = P - 1 - rng.integers(0, 40, (N, U)); A[:, 2, ::2] = v[:, 2, None, :]
    return pack(X, nb, v, A, y, j, z, w)
def check_inputs(d):
    bad = []
    for k, hi in (("x", 255), ("nb", P - 1), ("v0", P - 1), ("a0", P - 1), ("y0", 255), ("j0", U - 1), ("z0", 255), ("w", 4095)):
        a = np.asarray(d[k]).astype(np.float64)
        if not (np.min(a) >= 0 and np.max(a) <= hi): bad.append("range of " + k)
        elif not np.all(a == np.floor(a)): bad.append("whole numbers of " + k)
    return bad
def pick(X, k):
    return np.take_along_axis(X, k[:, :, None, :], 3)
def far(X, K, y):
    return np.stack([np.sum(np.abs(pick(X, K[:, :, l]) - y), axis=2) for l in range(16)], axis=2)
def reference(x, nb, v0, a0, y0, j0, z0, w):
    def vec(a): return a.astype(np.float32).astype(np.int64).reshape(N, 8, 16, -1)
    X, y, z = vec(x), vec(y0), vec(z0); nbr, A, W = (a.astype(np.int64).reshape(N, 8, 16, -1) for a in (nb, a0, w))
    v, j = v0.astype(np.int64), j0.astype(np.int64); lv = np.arange(1, 17)[None, None, :, None]
    tr = np.tile(np.arange(P), (N, 8, 1)); finds = np.zeros(N, np.int64)
    for t in range(1, RO + 1):
        n = pick(nbr, v); k = np.argmin(far(X, n, y), axis=2)
        v2 = np.take_along_axis(n, k[:, :, None, :], 2)[:, :, 0]; xn = pick(X, v2)
        new = far(X, A, xn) > TH * lv + 16 * (finds & 15)[:, None, None, None]
        top = 15 - np.argmax(new[:, :, ::-1], axis=2); some = np.any(new, axis=2)
        old = np.take_along_axis(A, top[:, :, None, :], 2)[:, :, 0]; xw = (xn + y) >> 1
        for r in range(N):
            for g in range(8):
                o = old[r, g][some[r, g]]; tr[r, g, o] = o
                q, i = np.unique(v[r, g], return_index=True); tr[r, g, q] = v2[r, g, i]
                q, i = np.unique(v2[r, g], return_index=True); X[r, g][:, q] = xw[r, g][:, i]
        A = np.where(new, v2[:, :, None, :], A); y = np.abs(y - xn); v = v2
        zz, jj = np.roll(z, t, axis=0), np.roll(j, t, axis=0)
        u = np.sum(W * zz, axis=2) & 4095; B = pick(A, jj)
        h = (((B * u[:, :, None, :]) >> 5) + B) & (P - 1)
        hit = far(X, h, zz) <= PH * lv
        l = np.where(np.any(hit, axis=2), np.argmax(hit, axis=2), 15)
        p = np.take_along_axis(B, l[:, :, None, :], 2)[:, :, 0]
        for c in range(3): p = np.take_along_axis(tr, p, 2)
        xp = pick(X, p); found = p == np.take_along_axis(v, jj, 2)
        zz = np.where(found[:, :, None, :], (zz + xp) >> 1, np.abs(zz - xp)); jj = np.where(found, u & (U - 1), jj)
        finds = np.sum(found, axis=(1, 2)); z, j = np.roll(zz, -t, axis=0), np.roll(jj, -t, axis=0)
    return {"yv": v.astype(np.float32), "ya": A.reshape(N, 128, U).astype(np.float32), "yy": y.reshape(N, 128, U).astype(np.float32).astype(BF),
            "yj": j.astype(np.float32), "yz": z.reshape(N, 128, S).astype(np.float32).astype(BF), "yt": tr.astype(np.float32)}

@@ -1,0 +1,783 @@
+import numpy as np
+from concourse.mybir import AluOpType, ActivationFunctionType
+
+AL = AluOpType
+AF = ActivationFunctionType
+NP, NU, NS, RO = 2048, 128, 256, 3
+XW = 2192
+HS = NS // 2
+PW = HS + 8
+MOVES = 2 * (RO + 1)
+TRI = 576
+SPARE = 2056
+F32, BF, F16, I32, U16 = "float32", "bfloat16", "float16", "int32", "uint16"
+
+SCRATCH = {
+    "X": ("sbuf", [128, XW], BF), "NB": ("sbuf", [128, NP], I32), "TR": ("sbuf", [128, XW + 8], F32),
+    "ld_v": ("sbuf", [128, NU], I32), "ld_j": ("sbuf", [128, NS], I32), "ld_a": ("sbuf", [128, NU], I32),
+    "ld_w": ("sbuf", [128, 4], I32), "jh": ("sbuf", [128, NS], F16),
+    "Y": ("sbuf", [128, NU], BF), "A": ("sbuf", [128, 2 * NU], F32), "A16": ("sbuf", [128, NU], U16), "T3": ("sbuf", [128, XW], F32),
+    "snd": ("sbuf", [128, MOVES * PW], BF), "rcv": ("sbuf", [128, (MOVES - 2) * PW], BF),
+    "hop": ("dram", [MOVES, 128, PW], BF), "home": ("dram", [2, 128, PW], BF),
+    "xi": ("sbuf", [128, 144], F32), "xp": ("sbuf", [128, 128], F32), "x16": ("sbuf", [128, 128], F32), "xm": ("sbuf", [128, 128], F32),
+    "ci": ("sbuf", [128, 16], I32), "cf": ("sbuf", [128, 16], F32),
+    "cb": ("sbuf", [128, 1920], BF), "ch": ("sbuf", [128, 1296], F16), "tht": ("sbuf", [128, 128], F32),
+    "cum": ("sbuf", [128, NS], F16), "vn": ("sbuf", [128, 8], F32), "bn": ("sbuf", [128, 8], F32), "c32": ("sbuf", [128, 784], F32),
+    "CT": ("sbuf", [128, TRI], BF), "eo": ("sbuf", [128, 2], U16),
+    "n16": ("sbuf", [128, NU], U16), "n32": ("sbuf", [128, NU], F32),
+    "g1": ("sbuf", [128, NP], BF), "g2": ("sbuf", [128, NP], BF), "e1": ("sbuf", [128, NP], BF), "e2": ("sbuf", [128, NP], BF),
+    "pm": ("sbuf", [128, NU], F32), "eqT": ("sbuf", [128, NU], BF), "sel": ("sbuf", [128, NU], F16),
+    "vr": ("sbuf", [128, 4 * NU], F32), "vh": ("sbuf", [128, NU], F16), "vw": ("sbuf", [128, 32], U16), "vf": ("sbuf", [128, 8], F32),
+    "vo": ("sbuf", [128, 32], U16), "xn": ("sbuf", [128, NU], BF), "xw": ("sbuf", [128, NU], I32),
+    "df": ("sbuf", [128, NU], F32), "nw": ("sbuf", [128, NU], F16), "nd": ("sbuf", [128, NU], F32),
+    "sb": ("sbuf", [128, NU], F16), "br": ("sbuf", [128, NU], F32), "bh": ("sbuf", [128, NU], F16), "bfw": ("sbuf", [128, 8], F32),
+    "bo": ("sbuf", [128, 8], U16),
+    "eq0": ("sbuf", [128, TRI], BF), "sc0": ("sbuf", [128, TRI], BF), "da0": ("sbuf", [128, 16], F32), "db0": ("sbuf", [128, 8], F32),
+    "eq1": ("sbuf", [128, TRI], BF), "sc1": ("sbuf", [128, TRI], BF), "da1": ("sbuf", [128, 16], F32), "db1": ("sbuf", [128, 8], F32),
+    "j16": ("sbuf", [128, 16], U16), "u1": ("sbuf", [128, NS], I32), "u2": ("sbuf", [128, NS], I32), "h16": ("sbuf", [128, NS], U16),
+    "Bh": ("sbuf", [128, NS], F16), "vj": ("sbuf", [128, NS], F32),
+    "g3": ("sbuf", [128, 2 * NP], BF), "e3": ("sbuf", [128, 2 * NP], BF),
+    "hit": ("sbuf", [128, NS], F16), "ss": ("sbuf", [128, NS], F16), "pw": ("sbuf", [128, 64], U16),
+    "m1": ("sbuf", [128, NS], F16), "m2": ("sbuf", [128, NS], F16), "fd": ("sbuf", [128, NS], BF),
+    "scl": ("sbuf", [128, NS], F32), "zz": ("sbuf", [128, NS], BF), "tz": ("sbuf", [128, NS], F32), "zi": ("sbuf", [128, NS], I32),
+    "w1": ("sbuf", [128, 16], I32), "w2": ("sbuf", [128, 16], I32), "dw": ("sbuf", [128, 16], F32), "tw": ("sbuf", [128, 16], F32),
+    "jr": ("sbuf", [128, NS], BF), "jb": ("sbuf", [128, 16], F32),
+    "fa": ("sbuf", [128, 4], F32), "fi": ("sbuf", [128, 4], I32), "th": ("sbuf", [128, 4], F32),
+    "PD0": ("psum", [128, 512], F32), "PD1": ("psum", [128, 512], F32), "PO": ("psum", [128, 512], F32), "PS0": ("psum", [128, 512], F32),
+    "PK": ("psum", [128, 512], F32), "PU": ("psum", [128, 512], F32), "PS1": ("psum", [128, 512], F32), "PN": ("psum", [128, 512], F32),
+}
+LOADS = ["v", "x", "nb", "a", "y", "j", "z", "z1", "w"]
+STORES = ["yv", "ya", "yy", "yt", "yz0", "yz1", "yj0", "yj1"]
+SEMAPHORES = (["dve", "act", "pe", "pool", "left"] + ["l_" + n for n in LOADS] + ["s_" + n for n in STORES]
+              + ["arr%d" % t for t in range(MOVES)] + ["rel%d" % t for t in range(MOVES)])
+WHOLE = ("PD0", "PD1", "PK", "PU")
+
+SL0 = {1: [8, 12], 2: [8, 12], 3: [8, 12]}
+OPT = {"tr3": 1, "xn1": 0, "xn2": 0, "xn3": 0}
+REV = True
+UL1 = {1: 8, 2: 16, 3: 16}
+UL2 = {1: 8, 2: 8, 3: 8}
+G1 = {1: "avva", 2: "aaaa", 3: "aaaa"}
+G2 = {1: "aaaa", 2: "aavv", 3: "aavv"}
+G3 = {1: "avavavav", 2: "avavavav", 3: "avavavav"}
+NA = [{0: 0, 1: 0, 2: 3, 3: 3}, {2: 3, 3: 3}]
+RELU = "a"
+PAIR = 2
+EARLY = (0.0, 100.0, 100.0)
+SEED, TILT, URGE, TURNS = 3, 0.15, 0.0, 3000
+CY, GA, SCAT, PECY, LAT, MOVE = 0.001, 1.56, 3.8, 0.0005, 0.1, 5.0
+
+
+def B(name, lo=0, hi=None, step=1):
+    return ("b", name, lo, SCRATCH[name][1][-1] if hi is None else hi, step)
+
+
+def IX(win, off):
+    return ("i", win, off)
+
+
+def cnt(a):
+    if a[0] == "i":
+        return 16 * (a[2][3] - a[2][2])
+    return (a[3] - a[2] + a[4] - 1) // a[4]
+
+
+def isap(a):
+    return isinstance(a, tuple)
+
+
+def ap(T, a):
+    if not isap(a):
+        return a
+    if a[0] == "i":
+        return ap(T, a[1]).indirect(ap(T, a[2]))
+    if a[4] == 1:
+        return T[a[1]][:, a[2]:a[3]]
+    return T[a[1]][:, a[2]:a[3]:a[4]]
+
+
+def wide(a):
+    return 2 if SCRATCH[a[1]][2] in (BF, F16, U16) else 4
+
+
+def psum(a):
+    return a[0] == "b" and SCRATCH[a[1]][0] == "psum"
+
+
+def build():
+    ops = []
+    acc = {}
+
+    def add(eng, ins, outs, inps, cost, **kw):
+        rd, wr = [], []
+        for a in inps:
+            if isap(a):
+                rd.extend([a[1], a[2]] if a[0] == "i" else [a])
+        for a in outs:
+            if a[0] == "i":
+                wr.append(a[1])
+                rd.append(a[2])
+            else:
+                wr.append(a)
+        me = len(ops)
+        deps = set(kw.get("after", []))
+        for lst, w in ((rd, False), (wr, True)):
+            for a in lst:
+                lo, hi = (0, 1 << 20) if a[1] in WHOLE else (a[2], a[3])
+                for (o, l2, h2, w2) in acc.get(a[1], []):
+                    if (w or w2) and l2 < hi and lo < h2:
+                        deps.add(o)
+        for lst, w in ((rd, False), (wr, True)):
+            for a in lst:
+                lo, hi = (0, 1 << 20) if a[1] in WHOLE else (a[2], a[3])
+                acc.setdefault(a[1], []).append((me, lo, hi, w))
+        deps.discard(me)
+        if kw.get("grp") is not None:
+            deps = set(d for d in deps if ops[d].get("grp") != kw["grp"] or ops[d].get("opens"))
+        o = {"eng": eng, "ins": ins, "deps": deps, "cost": cost, "banks": set(a[1] for a in rd + wr if psum(a)),
+             "name": "%s<-%s" % (outs[0][1] if outs and outs[0][0] == "b" else "ix", ",".join(str(a[1]) for a in rd[:2]))}
+        o.update(kw)
+        ops.append(o)
+        return me
+
+    def vc(n, out, ins, f=1.0):
+        if out[0] == "i":
+            return 0.05 + n * SCAT * CY
+        if ins[0][0] == "i":
+            return 0.05 + n * GA * CY
+        return 0.04 + max(64, n * f) * CY
+
+    def half(*aps):
+        return 0.5 if all(a[0] == "b" and wide(a) == 2 for a in aps) else 1.0
+
+    def i_ts(out, in0, s1, s2, op0, op1=None):
+        if op1 is None:
+            return lambda g, T: g.vector.tensor_scalar(ap(T, out), ap(T, in0), ap(T, s1), None, op0)
+        return lambda g, T: g.vector.tensor_scalar(ap(T, out), ap(T, in0), ap(T, s1), ap(T, s2), op0, op1)
+
+    def ts(out, in0, s1, s2, op0, op1=None):
+        return add(["dve"], {"dve": [i_ts(out, in0, s1, s2, op0, op1)]}, [out], [in0, s1, s2],
+                   {"dve": vc(cnt(in0), out, [in0], half(out, in0))})
+
+    def tsm(calls):
+        return add(["dve"], {"dve": [i_ts(*c) for c in calls]}, [c[0] for c in calls], [a for c in calls for a in c[1:4]],
+                   {"dve": sum(vc(cnt(c[1]), c[0], [c[1]], half(c[0], c[1])) for c in calls)})
+
+    def tt(out, in0, in1, op):
+        f = 1.0 if (psum(in0) or psum(in1)) else 2.0
+        return add(["dve"], {"dve": [lambda g, T: g.vector.tensor_tensor(ap(T, out), ap(T, in0), ap(T, in1), op)]}, [out], [in0, in1],
+                   {"dve": vc(cnt(in1), out, [in0], f)})
+
+    def scan(out, d0, d1, op0, op1):
+        return add(["dve"], {"dve": [lambda g, T: g.vector.tensor_tensor_scan(ap(T, out), ap(T, d0), ap(T, d1), 0.0, op0, op1)]},
+                   [out], [d0, d1], {"dve": vc(cnt(d0), out, [d0], half(out, d0, d1))})
+
+    def ms(out, val):
+        return add(["dve"], {"dve": [lambda g, T: g.vector.memset(ap(T, out), val)]}, [out], [], {"dve": vc(cnt(out), out, [out], 0.5)})
+
+    def ac(n, in_):
+        return 0.1 + n * (GA if in_[0] == "i" else 1.0) * CY
+
+    def act(out, in_, func, bias=0.0, scale=1.0, accum=None):
+        def f(g, T):
+            if accum is not None:
+                return g.scalar.activation(ap(T, out), ap(T, in_), func, bias=ap(T, bias), scale=scale, accum_out=ap(T, accum))
+            if func == AF.Copy:
+                return g.scalar.activation(ap(T, out), ap(T, in_), func, scale=scale)
+            return g.scalar.activation(ap(T, out), ap(T, in_), func, bias=ap(T, bias), scale=scale)
+        return add(["act"], {"act": [f]}, [out] + ([accum] if accum else []), [in_, bias], {"act": ac(cnt(in_), in_)})
+
+    def cp(out, in_, engs=("dve",)):
+        n = cnt(in_)
+        return add(list(engs), {"dve": [lambda g, T: g.vector.tensor_copy(ap(T, out), ap(T, in_))],
+                                "act": [lambda g, T: g.scalar.activation(ap(T, out), ap(T, in_), AF.Copy)]},
+                   [out], [in_], {"dve": vc(n, out, [in_], half(out, in_)), "act": ac(n, in_)})
+
+    def mm(calls, **kw):
+        calls = [list(c) for c in calls]
+
+        def one(c):
+            return lambda g, T: g.tensor.matmul(ap(T, c[0]), ap(T, c[1]), ap(T, c[2]), c[3], c[4])
+        cost = 0.05 + sum(max(min(64, cnt(c[1])), cnt(c[2])) * (4 if wide(c[1]) == 4 else 1) * PECY for c in calls)
+        return add(["pe"], {"pe": [one(c) for c in calls]}, [c[0] for c in calls], [a for c in calls for a in c[1:3]], {"pe": cost},
+                   calls=calls, **kw)
+
+    def iota(out, pattern, base, cm):
+        def f(g, T):
+            if SCRATCH[out[1]][2] == I32:
+                return g.iota(ap(T, out), pattern, base, cm)
+            return g.iota(ap(T, out), pattern, base, cm, allow_small_or_imprecise_dtypes=True)
+        return add(["pool"], {"pool": [f]}, [out], [], {"pool": 0.13 + 2 * cnt(out) * CY})
+
+    def select(out, in_, pattern, cmp, fill, cm):
+        return add(["pool"], {"pool": [lambda g, T: g.affine_select(ap(T, out), ap(T, in_), pattern, cmp, fill, 0, cm)]},
+                   [out], [in_], {"pool": 0.17 + 2 * cnt(out) * CY})
+
+    def dma(q, sem, f, outs, inps, lat):
+        return add([q], {q: [f]}, outs, inps, {q: 0.1 if q != "pool" else 0.5}, sem=sem, lat=lat)
+
+    FLEX, ACT = ("act", "dve"), ("act",)
+    ms(B("ld_v"), 0)
+    ms(B("ld_j"), 0)
+    dma("sync", "l_v", lambda g, T: g.sync.dma_start(T.ld_v[0:128:16, :], T.v0[:]), [B("ld_v")], [], 2.0)
+    dma("sync", "l_x", lambda g, T: g.sync.dma_start(T.X[:, 0:NP], T.x[:]), [B("X", 0, NP)], [], 4.5)
+    dma("sync", "l_nb", lambda g, T: g.sync.dma_start(T.NB[:], T.nb[:]), [B("NB")], [], 8.0)
+    dma("act", "l_a", lambda g, T: g.scalar.dma_start(T.ld_a[:], T.a0[:]), [B("ld_a")], [], 2.5)
+    dma("act", "l_j", lambda g, T: g.scalar.dma_start(T.ld_j[0:128:16, :], T.j0[:]), [B("ld_j")], [], 2.8)
+    dma("act", "l_z", lambda g, T: g.scalar.dma_start(T.snd[:, 0:HS], T.z0[:, 0:HS]), [B("snd", 0, HS)], [], 3.2)
+    dma("act", "l_z1", lambda g, T: g.scalar.dma_start(T.snd[:, PW:PW + HS], T.z0[:, HS:NS]), [B("snd", PW, PW + HS)], [], 3.4)
+    dma("act", "l_y", lambda g, T: g.scalar.dma_start(T.Y[:], T.y0[:]), [B("Y")], [], 3.5)
+    iota(B("ci", 0, 1), [[0, 1]], 0, 1)
+    iota(B("xi"), [[1, 144]], 0, 0)
+    iota(B("xp"), [[1, 128]], 0, -1)
+    iota(B("x16"), [[16, 8], [0, 16]], 0, 0)
+    iota(B("xm"), [[0, 8], [1, 16]], 0, 0)
+    dma("pool", "l_w", lambda g, T: g.dma_start(T.ld_w[:, 0:1], T.w[:], allow_slow_non_contiguous=True), [B("ld_w")], [], 3.0)
+    ms(B("X", NP, XW), 0.0)
+
+    def col(name, c):
+        return B(name, c, c + 1)
+    G16, LC, THR, DC, C7, E1, WH, WL, W7 = (col("cf", c) for c in range(9))
+    tsm([(col("ci", 1), col("ci", 0), 112, None, AL.bitwise_and), (col("ci", 2), col("ci", 0), 15, None, AL.bitwise_and)])
+    cp(B("cf", 0, 2), B("ci", 1, 3))
+    tsm([(THR, LC, 85.0, 85.0, AL.mult, AL.add), (DC, LC, float(SPARE), -2.0, AL.add, AL.mult),
+         (C7, LC, 160.0, 15.0, AL.mult, AL.add), (E1, LC, -144.0, 1151.0, AL.mult, AL.add)])
+    ts(B("eo", 0, 1), E1, C7, 0.0, AL.min, AL.max)
+    names = ["I", "nI", "Kc", "WH", "WL", "zero", "nBu"]
+    cb = dict((n, B("cb", 128 * i, 128 * i + 128)) for i, n in enumerate(names))
+    ms(cb["zero"], 0.0)
+    mo = dict((n, 1024 + 144 * i) for i, n in enumerate(["M1", "M2", "Mn", "Ms", "Mw"]))
+    B16, B32, Bn16 = B("cb", 1744, 1752), B("cb", 1760, 1768), B("cb", 1776, 1784)
+    B1, B2, Bn1 = B("cb", 1792, 1800), B("cb", 1808, 1816), B("cb", 1824, 1832)
+    I16, Blk16, I8, TriU = (B("ch", 128 * i, 128 * i + 128) for i in range(4))
+    In4, THT = B("ch", 1168, 1296), B("tht")
+    MASK, SEG = B("ch", 512, 640), B("ch", 768, 896)
+    ONES, RST, BLK, t1, t2, t3, DUMP = (B("c32", 128 * i, min(128 * i + 128, 784)) for i in range(7))
+
+    def M(n, d):
+        if n == "h":
+            return B("ch", 1024 + 15 - d, 1024 + 143 - d)
+        return B("cb", mo[n] + 15 - d, mo[n] + 143 - d)
+
+    def MM(n):
+        return B("cb", mo[n], mo[n] + 144)
+    tsm([(B("ch", 1024, 1168), B("xi"), G16, 15.0, AL.subtract, AL.is_equal),
+         (Blk16, B("x16"), G16, None, AL.is_equal),
+         (MM("M1"), B("xi"), G16, 15.0, AL.subtract, AL.is_equal),
+         (BLK, B("x16"), G16, None, AL.is_equal),
+         (cb["I"], B("xp"), 0.0, None, AL.is_equal),
+         (cb["nI"], B("xp"), 0.0, -1.0, AL.is_equal, AL.mult),
+         (MASK, B("xm"), LC, None, AL.is_equal)])
+    act(MM("M2"), MM("M1"), AF.Copy, scale=2.0)
+    act(MM("Mn"), MM("M1"), AF.Copy, scale=-1.0)
+    act(MM("Ms"), MM("M1"), AF.Copy, scale=0.0625)
+    act(I16, cb["I"], AF.Copy)
+    act(cb["Kc"], B("xm", 0, 128), AF.Copy)
+    act(B16, B("c32", 256, 384, 16), AF.Copy, scale=16.0)
+    act(B32, B("c32", 256, 384, 16), AF.Copy, scale=32.0)
+    act(Bn16, B("c32", 256, 384, 16), AF.Copy, scale=-16.0)
+    ms(ONES, 1.0)
+    act(B1, B("c32", 256, 384, 16), AF.Copy)
+    act(B2, B("c32", 256, 384, 16), AF.Copy, scale=2.0)
+    act(Bn1, B("c32", 256, 384, 16), AF.Copy, scale=-1.0)
+    act(I8, cb["I"], AF.Copy, scale=8192.0)
+    act(In4, cb["I"], AF.Copy, scale=-4096.0)
+    offs = [144 * c if c < 4 else 160 * (7 - c) + 16 for c in range(8)]
+    ms(B("CT"), 0.0)
+    for c in range(8):
+        act(B("CT", offs[c] + 16 * c, offs[c] + 16 * c + 16), B("ch", 512, 528), AF.Copy, scale=-0.5)
+    ms(B("CT", 0, TRI, 144), 4096.0)
+    ms(B("CT", 16, TRI, 160), 4096.0)
+    tsm([(DUMP, B("xi", 0, 16), -32.0, DC, AL.mult, AL.add), (RST, B("xm", 0, 128), 0.0, 1000000.0, AL.is_equal, AL.mult),
+         (SEG, B("xm"), 0.0, None, AL.not_equal)])
+    act(THT, B("xm"), AF.Identity, bias=85.0, scale=85.0)
+    ts(t1, B("xm", 0, 128), float(min(UL2.values())), -1.0, AL.is_ge, AL.mult)
+    tt(cb["nBu"], t1, BLK, AL.mult)
+    act(t2, BLK, AF.Copy, scale=-4096.0)
+    select(t3, t2, [[-1, 128]], AL.is_gt, 0.0, 1)
+    select(TriU, t3, [[-1, 128]], AL.not_equal, 4096.0, 1)
+    iota(B("TR"), [[1, XW + 8]], -8, 0)
+    if OPT["tr3"]:
+        iota(B("T3"), [[1, XW]], 0, 0)
+    tsm([(col("ci", 4), col("ld_w", 0), 4080, None, AL.bitwise_and), (col("ci", 5), col("ld_w", 0), 15, None, AL.bitwise_and),
+         (col("ci", 6), col("ld_w", 0), 127, None, AL.bitwise_and)])
+    cp(B("cf", 6, 9), B("ci", 4, 7))
+    tsm([(cb["WH"], BLK, WH, None, AL.mult), (cb["WL"], BLK, WL, None, AL.mult), (MM("Mw"), MM("M1"), W7, None, AL.mult)])
+
+    def wrap(out, m, src, n, block=False):
+        lo = src[2]
+        return mm([(out, M(m, d), B(src[1], lo + n * d, lo + n * d + n) if block else B(src[1], lo + d, src[3], 16), d == 0, d == 15)
+                   for d in range(16)])
+
+    def send(t):
+        s = add(["pool"], {"pool": ["send"]}, [], [B("snd", t * PW, t * PW + PW)], {"pool": 1.0}, t=t, sem="left", lat=1.0)
+        out = B("rcv", t * PW, t * PW + PW) if t < 2 * RO else col("home", t - 2 * RO)
+        return add(["none"], {}, [out], [], {"none": MOVE}, sem="arr%d" % t, after=[s], lat=0.0)
+
+    def lowest(k, rep16, wf, wn, out, shift, na):
+        eq, sc, da, db = "eq%d" % k, "sc%d" % k, "da%d" % k, "db%d" % k
+        for c in range(8):
+            o, i = B(eq, offs[c], offs[c] + 16 * c + 16), B(rep16[1], rep16[2], rep16[2] + 16 * c + 16)
+            if c >= 8 - na:
+                act(o, i, AF.Abs, bias=B(wn[1], c, c + 1))
+            else:
+                ts(o, i, B(wf[1], c, c + 1), None, AL.not_equal)
+        scan(B(sc), B("CT"), B(eq), AL.add, AL.min)
+        tt(B(da), IX(B(sc), B("eo", 0, 1)), DUMP, AL.mult)
+        tt(B(db), B(da, 0, 8), wf, AL.max)
+        ts(out, B(db), float(shift), None, AL.add)
+
+    def place_lists(t):
+        mm([(B("PN", 0, 128), Blk16, B("sel"), True, True)])
+        wrap(B("PN", 384, 392), "h", B("sel"), 8)
+        cp(B("vw", 8 * t, 8 * t + 8), B("PN", 384, 392))
+        cp(B("vf"), B("PN", 384, 392))
+        if NA[0][t]:
+            act(B("vn"), B("vf"), AF.Copy, scale=-1.0)
+        cp(B("vr", NU * t, NU * t + NU), B("PN", 0, 128), ACT)
+        lowest(0, B("vr", NU * t), B("vf"), B("vn"), B("vo", 8 * t, 8 * t + 8), 0, NA[0][t])
+
+    def gather(dst, lst, n, who, s0=0):
+        k = n // len(who)
+        for q, e in enumerate(who):
+            c = s0 + q * k
+            cp(B(dst, 16 * c, 16 * (c + k)), IX(B("X", 0, NP), B(lst, c, c + k)), {"a": ACT, "v": ("dve",), "f": FLEX}[e])
+
+    flip = [0]
+
+    def dists(src, tmp, n, opnd, opP, l0, nl, first, red, s0=0, grp=None, more=()):
+        per = 512 // n
+        steps = []
+        for c in range(0, l0, per):
+            steps.append(("a", list(range(c, min(c + per, l0)))))
+        vs = [("v", list(range(l, min(l + PAIR, nl)))) for l in range(l0, nl, PAIR)]
+        order = []
+        while steps or vs:
+            for _ in range(per // PAIR):
+                if vs:
+                    order.append(vs.pop(0))
+            if steps:
+                order.append(steps.pop(0))
+        if l0 < nl:
+            mm([(opP, cb["I"], opnd, True, True)])
+        if grp is None:
+            grp = len(ops)
+        if first:
+            mm(first, grp=grp, opens=True)
+
+        def a(l):
+            return B(src, 16 * s0 + l, 16 * (s0 + n), 16)
+        for c in more:
+            mm([c + (False, False)], grp=grp)
+        for c in range(l0, nl, 4):
+            mm([x + (False, False) for l in range(c, min(c + 4, nl)) for x in red(l, "v", None, a(l))[1:]], grp=grp)
+        for i, (path, ls) in enumerate(order):
+            tile = B(tmp, 16 * s0 + ls[0] * n, 16 * s0 + (ls[-1] + 1) * n)
+            if path == "a":
+                bank = "PD%d" % flip[0]
+                flip[0] ^= 1
+                calls = []
+                for q, l in enumerate(ls):
+                    o = B(bank, q * n, q * n + n)
+                    calls += [(o, cb["I"], a(l), True, False), (o, cb["nI"], opnd, False, True)]
+                mm(calls)
+                act(tile, B(bank, 0, len(ls) * n), AF.Abs)
+            else:
+                for l in ls:
+                    tt(B(tmp, 16 * s0 + l * n, 16 * s0 + l * n + n), a(l), opP, AL.max)
+            mm([red(l, path, B(tmp, 16 * s0 + l * n, 16 * s0 + l * n + n), a(l))[0] + (False, False) for l in ls], grp=grp)
+        return grp
+
+    cp(B("sel"), B("ld_v"))
+    place_lists(0)
+    def aold(t):
+        return B("A", NU * (1 - (t & 1)), NU * (1 - (t & 1)) + NU)
+    act(t1, cb["I"], AF.Copy)
+    cp(aold(1), B("ld_a"))
+    cp(B("A16"), B("ld_a"))
+    cp(B("jh"), B("ld_j"))
+    wrap(B("PS0", 0, 16), "h", B("jh"), 16)
+    for hf in range(2):
+        cp(B("snd", hf * PW + HS, hf * PW + PW), B("PS0", 8 * hf, 8 * hf + 8))
+        send(hf)
+    for o in ops:
+        o["boost"] = EARLY[0] if o["eng"] == ["act"] or o["name"][:2] in ("TR", "T3") else EARLY[1]
+
+    def users_a(t):
+        vw_old, vw = B("vw", 8 * t - 8, 8 * t), B("vw", 8 * t, 8 * t + 8)
+        cp(B("n16"), IX(B("NB"), vw_old))
+        cp(B("n32"), B("n16"))
+        k = len(ops)
+        gather("g2", "A16", NU, G2[t])
+        for o in ops[k:]:
+            o["boost"] = EARLY[2] if t == 1 else 0.0
+        gather("g1", "n16", NU, G1[t])
+
+        def red1(k, path, tile, a):
+            o = B("PK", k, 128, 16)
+            if path == "a":
+                return [(o, tile, B16)]
+            return [(o, tile, B32), (o, a, Bn16), (o, B("Y"), Bn16)]
+        dists("g1", "e1", NU, B("Y"), B("PO", 256, 384), UL1[t], 16, [(B("PK", 0, 128), cb["I"], cb["Kc"], True, False)], red1)
+        scan(B("pm"), RST, B("PK", 0, 128), AL.add, AL.min)
+        if REV:
+            add(["dve"], {"dve": [lambda g, T: g.vector.tensor_tensor_scan(T.df[:, ::-1], ap(T, RST), T.pm[:, ::-1], 0.0, AL.add, AL.min)]},
+                [B("df")], [RST, B("pm")], {"dve": 0.04 + 128 * CY})
+            tt(B("eqT"), B("PK", 0, 128), B("df"), AL.is_equal)
+        else:
+            tsm([(B("eqT", 16 * q, 16 * q + 16), B("PK", 16 * q, 16 * q + 16), col("pm", 16 * q + 15), None, AL.is_equal)
+                 for q in range(8)])
+        mm([(B("PK", 128, 256), B("eqT"), cb["I"], True, True)])
+        tt(B("sel"), B("PK", 128, 256), B("n32"), AL.mult)
+        place_lists(t)
+        cp(B("xn"), IX(B("X", 0, NP), vw), ACT if OPT["xn%d" % t] else ("dve",))
+
+        def red2(l, path, tile, a):
+            o = B("PU", 0, 128)
+            if path == "a":
+                return [(o, M("M1", l), tile)]
+            return [(o, M("M2", l), tile), (o, M("Mn", l), a)]
+        more = [(B("PU", 0, 128), cb["nBu"], B("xn"))] if UL2[t] < 16 else []
+        dists("g2", "e2", NU, B("xn"), B("PO", 384, 512), UL2[t], 16, [], red2, more=more)
+        tt(B("PK", 256, 384), B("PN", 0, 128), aold(t), AL.subtract)
+        mm([(B("PN", 128, 256), cb["I"], B("xn"), True, False), (B("PN", 128, 256), cb["I"], B("Y"), False, True),
+            (B("PN", 256, 384), cb["I"], B("xn"), True, False), (B("PN", 256, 384), cb["nI"], B("Y"), False, True)])
+        ts(B("xw"), B("PN", 128, 256), 0.5, -0.25, AL.mult, AL.add)
+        act(B("Y"), B("PN", 256, 384), AF.Abs)
+
+    def users_b(t):
+        cp(IX(B("X"), B("vo", 8 * t, 8 * t + 8)), B("xw"))
+        ts(B("nw"), B("PU", 0, 128), THR if t == 1 else col("th", 0), None, AL.is_gt)
+        tt(B("PK", 384, 512), B("nw"), B("PK", 256, 384), AL.mult)
+        tt(B("A", NU * (t & 1), NU * (t & 1) + NU), aold(t), B("PK", 384, 512), AL.add)
+        if t > 1:
+            mm([(B("PU", 128, 256), t1, aold(t), True, False), (B("PU", 128, 256), TriU, B("nw"), False, True)])
+            ts(B("sb"), B("PU", 128, 256), -4095.0, 0.0, AL.add, AL.max)
+            mm([(B("PU", 256, 384), Blk16, B("sb"), True, True)])
+            wrap(B("PU", 384, 392), "h", B("sb"), 8)
+            cp(B("bfw"), B("PU", 384, 392))
+            if NA[1][t]:
+                act(B("bn"), B("bfw"), AF.Copy, scale=-1.0)
+            cp(B("br"), B("PU", 256, 384), ACT)
+            lowest(1, B("br"), B("bfw"), B("bn"), B("bo"), 7, NA[1][t])
+            ts(IX(B("TR"), B("bo")), B("br"), 1.0, -1.0, AL.mult, AL.add)
+        cp(IX(B("TR", 8), B("vo", 8 * t - 8, 8 * t)), B("vr", NU * t, NU * t + NU))
+        if t == 1 and OPT["tr3"]:
+            tt(B("sb"), IX(B("TR", 8, 8 + NP), B("vw", 8, 16)), MASK, AL.mult)
+            scan(B("bh"), SEG, B("sb"), AL.mult, AL.max)
+            cp(B("bo"), B("bh", 15, NU, 16))
+            cp(B("br"), IX(B("TR", 8, 8 + NP), B("bo")), ACT)
+            cp(IX(B("T3"), B("vo", 0, 8)), B("br"))
+        if t < RO:
+            cp(B("A16"), aold(t + 1))
+        else:
+            dma("sync", "s_yv", lambda g, T: g.sync.dma_start(T.yv[:], T.vr[0:128:16, NU * RO:NU * RO + NU]), [], [B("vr", NU * RO)], 2.0)
+            dma("sync", "s_ya", lambda g, T: g.sync.dma_start(T.ya[:], ap(T, aold(RO + 1))), [], [aold(RO + 1)], 2.0)
+            dma("sync", "s_yy", lambda g, T: g.sync.dma_start(T.yy[:], T.Y[:]), [], [B("Y")], 2.0)
+            dma("sync", "s_yt", lambda g, T: g.sync.dma_start(T.yt[:], T.TR[0:128:16, 8:8 + NP]), [], [B("TR")], 2.5)
+
+    def seekers(t, hf):
+        lo, hi, c8 = HS * hf, HS * hf + HS, 8 * hf
+        r0, s0 = (2 * t - 2 + hf) * PW, (2 * t + hf) * PW
+        z, jw = B("rcv", r0, r0 + HS), B("rcv", r0 + HS, r0 + PW)
+        last, bank = t == RO, "PS%d" % hf
+        TRW, XS = B("TR", 8, 8 + NP), B("X", 0, NP)
+
+        def H(name):
+            return B(name, lo, hi)
+
+        def W(name):
+            return B(name, c8, c8 + 8)
+        pu, pt, pz = B(bank, 0, HS), B(bank, HS, 2 * HS), B("PO", lo, hi)
+        cp(W("j16"), jw)
+        mm([(pu, cb["WH"], z, True, False), (pu, cb["WL"], z, False, True)])
+        cp(H("Bh"), IX(aold(t + 1), W("j16")), ACT)
+        cp(H("u1"), pu)
+        ts(H("u2"), H("u1"), 4095, None, AL.bitwise_and)
+        ts(pu, H("u2"), 32.0, None, AL.add)
+        tt(H("u2"), H("Bh"), pu, AL.mult)
+        ts(H("u1"), H("u2"), 5, 2047, AL.arith_shift_right, AL.bitwise_and)
+        cp(H("h16"), H("u1"))
+        gather("g3", "h16", HS, G3[t][4 * hf:4 * hf + 4], lo)
+        cp(H("vj"), IX(B("vr", NU * t, NU * t + NU), W("j16")), ACT)
+        wrap(B("PN", 432 + c8, 440 + c8), "Mw", z, 8, last)
+        cp(W("w1"), B("PN", 432 + c8, 440 + c8))
+        ts(W("w2"), W("w1"), 127, None, AL.bitwise_and)
+        if last:
+            cp(H("jr"), IX(B("xi", 0, 128), W("j16")), ACT)
+            wrap(B("PN", 448 + c8, 456 + c8), "Ms", H("jr"), 8, True)
+            cp(W("jb"), B("PN", 448 + c8, 456 + c8))
+            jw = W("jb")
+        tt(W("dw"), W("w2"), jw, AL.subtract)
+
+        def red(l, path, tile, a):
+            o = B(bank, l, HS, 16)
+            if path == "a":
+                return [(o, tile, B1)]
+            return [(o, tile, B2), (o, a, Bn1), (o, z, Bn1)]
+        dists("g3", "e3", HS, z, pz, SL0[t][hf], 15, [(pu, cb["zero"], z, True, False)], red, lo)
+        tt(H("hit"), pu, THT, AL.is_le)
+        scan(H("cum"), SEG, H("hit"), AL.mult, AL.add)
+        mm([(pt, I16, H("Bh"), True, False), (pt, H("hit"), I8, False, False), (pt, H("cum"), In4, False, True)])
+        if RELU == "a":
+            act(H("ss"), pt, AF.Relu, bias=-4096.0)
+        else:
+            ts(H("ss"), pt, -4096.0, 0.0, AL.add, AL.max)
+        wrap(B(bank, 256, 264), "h", H("ss"), 8)
+        c0 = 0
+        if t == 1 and OPT["tr3"]:
+            c0, TRW = 2, B("T3", 0, NP)
+
+        def pw(c):
+            return B("pw", 32 * hf + 8 * c, 32 * hf + 8 * c + 8)
+        cp(pw(c0), B(bank, 256, 264))
+        for c in range(c0, 3):
+            tt(H("m1"), IX(TRW, pw(c)), MASK, AL.mult)
+            if c == 2:
+                tt(H("fd"), IX(TRW, pw(c)), H("vj"), AL.is_equal)
+            scan(H("m2"), SEG, H("m1"), AL.mult, AL.max)
+            cp(pw(c + 1), B("m2", lo + 15, hi, 16))
+        act(pt, H("fd"), AF.Identity, bias=1.0, scale=-2.0)
+        act(H("scl"), H("fd"), AF.Identity, bias=1.0, scale=-HALF, accum=None if last else col("fa", hf))
+        tt(H("zz"), pt, z, AL.mult)
+        tt(H("tz"), IX(XS, pw(3)), H("zz"), AL.subtract)
+        act(pu, H("tz"), AF.Abs)
+        tt(H("zi"), pu, H("scl"), AL.mult)
+        cp(B("snd", s0, s0 + HS), H("zi"))
+        wrap(B(bank, 272, 280), "Ms", H("fd"), 8, last)
+        tt(W("tw"), B(bank, 272, 280), W("dw"), AL.mult)
+        tt(B("snd", s0 + HS, s0 + PW), W("tw"), jw, AL.add)
+        send(2 * t + hf)
+
+    def finds():
+        o = B("PN", 464, 465)
+        mm([(o, ONES, col("fa", 0), True, False), (o, ONES, col("fa", 1), False, True)])
+        ts(col("fi", 0), o, -1.0 / HALF, 32768.0 / HALF, AL.mult, AL.add)
+        ts(col("fi", 1), col("fi", 0), 255, None, AL.bitwise_and)
+        ts(col("th", 0), col("fi", 1), THR, None, AL.add)
+
+    users_a(1)
+    users_b(1)
+    for t in range(1, RO + 1):
+        k = len(ops)
+        seekers(t, 0)
+        for o in ops[k:]:
+            o["boost"] = URGE
+        seekers(t, 1)
+        if t < RO:
+            finds()
+            users_a(t + 1)
+            users_b(t + 1)
+
+    def store(hf):
+        lo = HS * hf
+        dma("sync", "s_yz%d" % hf, lambda g, T: g.sync.dma_start(T.yz[:, lo:lo + HS], T.home[hf, :, 0:HS]), [], [col("home", hf)], 2.0)
+        dma("pool", "s_yj%d" % hf, lambda g, T: g.dma_start(T.yj[:, lo:lo + HS], T.home[hf, :, HS:PW]), [], [col("home", hf)], 2.5)
+    store(0)
+    store(1)
+    return ops
+
+
+HALF = 0.5 + 2.0 ** -11
+
+
+def schedule(ops):
+    n = len(ops)
+    succ = [[] for _ in ops]
+    for i, o in enumerate(ops):
+        for d in set(o["deps"]) | set(o.get("soft", [])):
+            succ[d].append(i)
+
+    pred = [sorted(set(o["deps"]) | set(o.get("soft", []))) for o in ops]
+    free_of = set((d, i) for i, o in enumerate(ops) for d in o.get("soft", []) if d not in o["deps"])
+    eng = [o["eng"][0] for o in ops]
+    cost = [o["cost"][e] for o, e in zip(ops, eng)]
+    lat = [o.get("lat", 0.0) for o in ops]
+
+    def sweep(before, after, prio, back):
+        left = [len(b) for b in before]
+        can = [0.0] * n
+        ready = [i for i in range(n) if left[i] == 0]
+        busy, done, at = {}, [0.0] * n, [0.0] * n
+        while ready:
+            i = max(ready, key=lambda x: prio[x])
+            e, st = eng[i], can[i]
+            held = [x for x in busy.get(e, []) if x[1] > st]
+            for b in ops[i]["banks"]:
+                held += [(x[0] - LAT, x[1] + LAT) for x in busy.get(b, []) if x[2] != e and x[1] + LAT > st]
+            for x in sorted(held):
+                if x[0] >= st + cost[i] - 1e-9:
+                    break
+                st = max(st, x[1])
+            at[i] = st
+            done[i] = st + cost[i] + (0.0 if back else lat[i])
+            if e != "none":
+                busy.setdefault(e, []).append((st, st + cost[i]))
+            for b in ops[i]["banks"]:
+                busy.setdefault(b, []).append((st, st + cost[i], e))
+            ready.remove(i)
+            for s in after[i]:
+                can[s] = max(can[s], done[i] + (0.0 if (e == "pe" and eng[s] == "pe") or (i, s) in free_of else LAT))
+                left[s] -= 1
+                if left[s] == 0:
+                    ready.append(s)
+        order = sorted(range(n), key=lambda x: (at[x], x))
+        bank, extra = {}, []
+        for i in order:
+            for b in ops[i]["banks"]:
+                if b in bank and eng[bank[b]] != eng[i]:
+                    extra.append((i, bank[b]))
+                bank[b] = i
+        return max(done), order, at, extra, done
+
+    prio = [0.0] * n
+    for i in reversed(sweep(pred, succ, prio, False)[1]):
+        prio[i] = cost[i] + lat[i] + LAT + max([prio[s] for s in succ[i]] + [0.0])
+    rng = np.random.default_rng(SEED)
+    prio = [p + o.get("boost", 0.0) for p, o in zip(prio, ops)]
+    best = now = sweep(pred, succ, prio, False)
+    for turn in range(TURNS):
+        _, order, at, extra, done = now
+        last, prev = {}, {}
+        for i in order:
+            prev[i] = last.get(eng[i]) if eng[i] != "none" else None
+            last[eng[i]] = i
+        held = dict(extra)
+        i, jams = max(range(n), key=lambda x: done[x]), []
+        while True:
+            d = max(pred[i], key=lambda x: done[x]) if pred[i] else None
+            t = done[d] + (0.0 if eng[i] == "pe" and eng[d] == "pe" else LAT) if d is not None else 0.0
+            if t < at[i] - 1e-6:
+                j = prev[i]
+                if i in held and (j is None or done[held[i]] + LAT > at[j] + cost[j]):
+                    j = held[i]
+                if j is not None:
+                    jams.append((i, j))
+                    d = j
+            if d is None:
+                break
+            i = d
+        p2 = list(prio)
+        for _ in range(1 + int(rng.integers(0, 2))):
+            i, j = jams[int(rng.integers(0, len(jams)))]
+            if rng.random() < 0.5:
+                p2[j] = min(p2[j], p2[i]) - float(rng.uniform(0.0, 3.0))
+            else:
+                top, todo = max(p2[i], p2[j]) + float(rng.uniform(0.0, 1.0)), [i]
+                while todo:
+                    x = todo.pop()
+                    if p2[x] < top:
+                        p2[x] = top
+                        todo.extend(pred[x])
+        new = sweep(pred, succ, p2, False)
+        if new[0] <= now[0] + TILT * (1.0 - turn / TURNS) * float(rng.random()):
+            now, prio = new, p2
+            if new[0] < best[0]:
+                best = new
+    for i, o in enumerate(ops):
+        o["on"], o["at"] = eng[i], best[2][i]
+    for i, d in best[3]:
+        ops[i]["deps"].add(d)
+    return best[1], best[0]
+
+
+PLAN = {}
+
+
+def plan():
+    if not PLAN:
+        PLAN["ops"] = build()
+        PLAN["order"], PLAN["span"] = schedule(PLAN["ops"])
+        sums = {}
+        for i in PLAN["order"]:
+            o = PLAN["ops"][i]
+            if o.get("grp") is not None:
+                sums.setdefault(o["grp"], []).append(o)
+        for part in sums.values():
+            part[0]["calls"][0][3] = True
+            part[-1]["calls"][-1][4] = True
+    return PLAN["ops"], PLAN["order"]
+
+
+def target(T, r, t):
+    n = len(T.cores)
+    return T.cores[(r + 1) % n] if t < 2 * RO else T.cores[(r - RO) % n]
+
+
+def relay(T, topo, r):
+    c = T.cores[r]
+    ok = [h for h in topo.cores_of(c) if h not in T.cores and all(topo.may_write(h, target(T, r, t)) for t in range(MOVES))]
+    return sorted(ok, key=lambda h: topo.die(h) != topo.die(c))[0]
+
+
+def width(mask):
+    return bin(mask).count("1")
+
+
+def rank_program(g, core, T, topo):
+    rank = T.rank_of(core)
+    n = len(T.cores)
+    ops, order = plan()
+    if rank is None:
+        for r in range(n):
+            if relay(T, topo, r) == core:
+                total = 0
+                for t in [ops[i]["t"] for i in order if "t" in ops[i]]:
+                    d = target(T, r, t)
+                    rid, pid = topo.addr(d, core)
+                    g.wait_ge(T.sem["rel%d" % t], width(topo.mask(T.cores[r], core)))
+                    out = T.rcv[:, t * PW:t * PW + PW] if t < 2 * RO else T.home[t - 2 * RO]
+                    g.remote_dma(out, T.hop[t], T.sem["arr%d" % t], T.sem.left, pid, rid, topo.mask(core, d))
+                    total += width(topo.mask(core, d))
+                g.wait_ge(T.sem.left, total)
+        return
+    h = relay(T, topo, rank)
+    queue = {"dve": g.vector, "act": g.scalar, "pe": g.tensor, "pool": g, "sync": g.sync}
+    count = {}
+    known = dict((q, {}) for q in queue)
+    token, clock = {}, {}
+    for i in order:
+        o = ops[i]
+        e = o["on"]
+        if e == "none":
+            t = int(o["sem"][3:])
+            src = (rank - 1) % n if t < 2 * RO else (rank + RO) % n
+            token[i] = (o["sem"], width(topo.mask(relay(T, topo, src), core)))
+            clock[i] = {token[i][0]: token[i][1]}
+            continue
+        need = {}
+        for d in o["deps"]:
+            if e == "pe" and ops[d]["on"] == "pe":
+                continue
+            s, c = token[d]
+            if c > need.get(s, (0, 0))[0]:
+                need[s] = (c, d)
+        for s, (c, d) in sorted(need.items(), key=lambda x: -x[1][1]):
+            if known[e].get(s, 0) < c:
+                queue[e].wait_ge(T.sem[s], c)
+                for s2, c2 in clock[d].items():
+                    known[e][s2] = max(known[e].get(s2, 0), c2)
+        ins = o["ins"][e]
+        if ins == ["send"]:
+            t = o["t"]
+            rid, pid = topo.addr(h, core)
+            m = topo.mask(core, h)
+            g.remote_dma(T.hop[t], T.snd[:, t * PW:t * PW + PW], T.sem["rel%d" % t], T.sem.left, pid, rid, m)
+            count["left"] = count.get("left", 0) + width(m)
+            token[i] = ("left", count["left"])
+        elif "sem" in o:
+            ins[0](g, T).then_inc(T.sem[o["sem"]], 16)
+            token[i] = (o["sem"], 16)
+            count[o["sem"]] = 16
+        else:
+            for q, f in enumerate(ins):
+                x = f(g, T)
+                if e != "pe" or q == len(ins) - 1:
+                    x.then_inc(T.sem[e], 1)
+                    count[e] = count.get(e, 0) + 1
+            token[i] = (e, count[e])
+        clock[i] = dict(known[e])
+        clock[i][token[i][0]] = token[i][1]
+    for s, c in sorted(count.items()):
+        if known["pool"].get(s, 0) < c:
+            (g.sync if s in ("s_yv", "s_ya", "s_yy", "s_yt", "s_yz0", "s_yz1") else g).wait_ge(T.sem[s], c)

@@ -1,14 +1,14 @@
 import numpy as np
-from concourse.mybir import AluOpType, ActivationFunctionType
+from concourse.mybir import AluOpType, ActivationFunctionType, AxisListType
 
 AL = AluOpType
 AF = ActivationFunctionType
 NP, NU, NS, RO = 2048, 128, 256, 3
 XW = 2192
+TRI = 576
 HS = NS // 2
 PW = HS + 8
 MOVES = 2 * (RO + 1)
-TRI = 576
 SPARE = 2056
 F32, BF, F16, I32, U16 = "float32", "bfloat16", "float16", "int32", "uint16"
 
@@ -21,28 +21,25 @@ SCRATCH = {
     "hop": ("dram", [MOVES, 128, PW], BF), "home": ("dram", [2, 128, PW], BF),
     "xi": ("sbuf", [128, 144], F32), "xp": ("sbuf", [128, 128], F32), "x16": ("sbuf", [128, 128], F32), "xm": ("sbuf", [128, 128], F32),
     "ci": ("sbuf", [128, 16], I32), "cf": ("sbuf", [128, 16], F32),
-    "cb": ("sbuf", [128, 1920], BF), "ch": ("sbuf", [128, 1296], F16), "tht": ("sbuf", [128, 128], F32),
-    "cum": ("sbuf", [128, NS], F16), "vn": ("sbuf", [128, 8], F32), "bn": ("sbuf", [128, 8], F32), "c32": ("sbuf", [128, 784], F32),
-    "CT": ("sbuf", [128, TRI], BF), "eo": ("sbuf", [128, 2], U16),
-    "n16": ("sbuf", [128, NU], U16), "n32": ("sbuf", [128, NU], F32),
+    "cb": ("sbuf", [128, 3600], BF), "ch": ("sbuf", [128, 1800], F16), "c32": ("sbuf", [128, 640], F32),
+    "n16": ("sbuf", [128, NU], U16), "nh": ("sbuf", [128, NU], F16),
     "g1": ("sbuf", [128, NP], BF), "g2": ("sbuf", [128, NP], BF), "e1": ("sbuf", [128, NP], BF), "e2": ("sbuf", [128, NP], BF),
     "pm": ("sbuf", [128, NU], F32), "eqT": ("sbuf", [128, NU], BF), "sel": ("sbuf", [128, NU], F16),
-    "vr": ("sbuf", [128, 4 * NU], F32), "vh": ("sbuf", [128, NU], F16), "vw": ("sbuf", [128, 32], U16), "vf": ("sbuf", [128, 8], F32),
-    "vo": ("sbuf", [128, 32], U16), "xn": ("sbuf", [128, NU], BF), "xw": ("sbuf", [128, NU], I32),
-    "df": ("sbuf", [128, NU], F32), "nw": ("sbuf", [128, NU], F16), "nd": ("sbuf", [128, NU], F32),
-    "sb": ("sbuf", [128, NU], F16), "br": ("sbuf", [128, NU], F32), "bh": ("sbuf", [128, NU], F16), "bfw": ("sbuf", [128, 8], F32),
-    "bo": ("sbuf", [128, 8], U16),
+    "vr": ("sbuf", [128, 4 * NU], F32), "vw": ("sbuf", [128, 32], U16),
+    "vo": ("sbuf", [128, 32], U16), "xn": ("sbuf", [128, NU], BF), "xw": ("sbuf", [128, NU], I32), "XV": ("sbuf", [128, NU], BF),
+    "df": ("sbuf", [128, NU], F32), "nw": ("sbuf", [128, NU], BF), "dA": ("sbuf", [128, NU], F32),
+    "sb": ("sbuf", [128, NU], F16), "br": ("sbuf", [128, 3 * NU], F32), "bo": ("sbuf", [128, 56], U16),
+    "t1": ("sbuf", [128, 3 * NU], F16), "t2": ("sbuf", [128, 3 * NU], F16), "CT": ("sbuf", [128, TRI], BF), "eo": ("sbuf", [128, 2], U16),
     "eq0": ("sbuf", [128, TRI], BF), "sc0": ("sbuf", [128, TRI], BF), "da0": ("sbuf", [128, 16], F32), "db0": ("sbuf", [128, 8], F32),
     "eq1": ("sbuf", [128, TRI], BF), "sc1": ("sbuf", [128, TRI], BF), "da1": ("sbuf", [128, 16], F32), "db1": ("sbuf", [128, 8], F32),
-    "j16": ("sbuf", [128, 16], U16), "u1": ("sbuf", [128, NS], I32), "u2": ("sbuf", [128, NS], I32), "h16": ("sbuf", [128, NS], U16),
-    "Bh": ("sbuf", [128, NS], F16), "vj": ("sbuf", [128, NS], F32),
+    "j16": ("sbuf", [128, 16], U16), "q": ("sbuf", [128, NS], I32), "u1": ("sbuf", [128, NS], I32), "u2": ("sbuf", [128, NS], I32),
+    "h16": ("sbuf", [128, NS], U16), "Bh": ("sbuf", [128, NS], F32), "Aj": ("sbuf", [128, NS], F32), "vj": ("sbuf", [128, NS], F16),
     "g3": ("sbuf", [128, 2 * NP], BF), "e3": ("sbuf", [128, 2 * NP], BF),
-    "hit": ("sbuf", [128, NS], F16), "ss": ("sbuf", [128, NS], F16), "pw": ("sbuf", [128, 64], U16),
+    "cum": ("sbuf", [128, 2 * PW], BF), "ss": ("sbuf", [128, NS], F16), "pw": ("sbuf", [128, 64], U16),
     "m1": ("sbuf", [128, NS], F16), "m2": ("sbuf", [128, NS], F16), "fd": ("sbuf", [128, NS], BF),
-    "scl": ("sbuf", [128, NS], F32), "zz": ("sbuf", [128, NS], BF), "tz": ("sbuf", [128, NS], F32), "zi": ("sbuf", [128, NS], I32),
+    "xj": ("sbuf", [128, NS], BF), "fe": ("sbuf", [128, NS], F16), "zz": ("sbuf", [128, NS], BF), "tz": ("sbuf", [128, NS], BF),
     "w1": ("sbuf", [128, 16], I32), "w2": ("sbuf", [128, 16], I32), "dw": ("sbuf", [128, 16], F32), "tw": ("sbuf", [128, 16], F32),
-    "jr": ("sbuf", [128, NS], BF), "jb": ("sbuf", [128, 16], F32),
-    "fa": ("sbuf", [128, 4], F32), "fi": ("sbuf", [128, 4], I32), "th": ("sbuf", [128, 4], F32),
+    "jr": ("sbuf", [128, NS], BF), "jb": ("sbuf", [128, 16], F32), "fa": ("sbuf", [128, 4], F32),
     "PD0": ("psum", [128, 512], F32), "PD1": ("psum", [128, 512], F32), "PO": ("psum", [128, 512], F32), "PS0": ("psum", [128, 512], F32),
     "PK": ("psum", [128, 512], F32), "PU": ("psum", [128, 512], F32), "PS1": ("psum", [128, 512], F32), "PN": ("psum", [128, 512], F32),
 }
@@ -50,22 +47,20 @@ LOADS = ["v", "x", "nb", "a", "y", "j", "z", "z1", "w"]
 STORES = ["yv", "ya", "yy", "yt", "yz0", "yz1", "yj0", "yj1"]
 SEMAPHORES = (["dve", "act", "pe", "pool", "left"] + ["l_" + n for n in LOADS] + ["s_" + n for n in STORES]
               + ["arr%d" % t for t in range(MOVES)] + ["rel%d" % t for t in range(MOVES)])
-WHOLE = ("PD0", "PD1", "PK", "PU")
 
-SL0 = {1: [8, 12], 2: [8, 12], 3: [8, 12]}
-OPT = {"tr3": 1, "xn1": 0, "xn2": 0, "xn3": 0}
-REV = True
-UL1 = {1: 8, 2: 16, 3: 16}
-UL2 = {1: 8, 2: 8, 3: 8}
-G1 = {1: "avva", 2: "aaaa", 3: "aaaa"}
-G2 = {1: "aaaa", 2: "aavv", 3: "aavv"}
-G3 = {1: "avavavav", 2: "avavavav", 3: "avavavav"}
-NA = [{0: 0, 1: 0, 2: 3, 3: 3}, {2: 3, 3: 3}]
-RELU = "a"
-PAIR = 2
-EARLY = (0.0, 100.0, 100.0)
-SEED, TILT, URGE, TURNS = 3, 0.15, 0.0, 3000
-CY, GA, SCAT, PECY, LAT, MOVE = 0.001, 1.56, 3.8, 0.0005, 0.1, 5.0
+CFG = {
+    "G1": {1: "avva", 2: "aaaa", 3: "aaaa"}, "G2": {1: "aaaa", 2: "aaaa", 3: "aaaa"},
+    "G3": {1: "avaaaava", 2: "avaaaava", 3: "avavavav"},
+    "D1": {1: "vavv", 2: "vvav", 3: "aaaa"}, "D2": {1: "vava", 2: "vvaa", 3: "vvva"},
+    "D3": {1: "vvaavvva", 2: "vvvavvva", 3: "vaaavvaa"},
+    "xn": {1: "v", 2: "v", 3: "a"}, "Bh": {1: "aa", 2: "aa", 3: "aa"}, "vj": {1: "aa", 2: "aa", 3: "aa"},
+    "xv": {1: "a", 2: "a", 3: "a"}, "xj": {1: "aa", 2: "aa", 3: "aa"}, "sb": {1: "a", 2: "a", 3: "a"},
+    "walk": (0.0, 6.0), "tr3": "100", "early": (0.0, 100.0, 100.0), "consts": "avva", "free": 0,
+    "seed": 3, "tilt": 0.15, "turns": 2500,
+}
+CY, LAT0, LAT1, MOVE = 0.00086, 0.18, 0.18, 2.0
+PRICE = {"v": (0.01, CY), "g": (0.05, 1.56 * CY), "s": (0.05, 3.8 * CY), "a": (0.06, CY), "ag": (0.065, 1.56 * CY),
+         "p0": (0.02, 0.0), "p": (0.0, 0.5 * CY)}
 
 
 def B(name, lo=0, hi=None, step=1):
@@ -74,6 +69,10 @@ def B(name, lo=0, hi=None, step=1):
 
 def IX(win, off):
     return ("i", win, off)
+
+
+def S(a, lo, hi=None, step=1):
+    return B(a[1], a[2] + lo, a[3] if hi is None else a[2] + hi, step)
 
 
 def cnt(a):
@@ -107,6 +106,7 @@ def psum(a):
 def build():
     ops = []
     acc = {}
+    C = CFG
 
     def add(eng, ins, outs, inps, cost, **kw):
         rd, wr = [], []
@@ -119,33 +119,40 @@ def build():
                 rd.append(a[2])
             else:
                 wr.append(a)
+        banks = set(a[1] for a in rd + wr if psum(a))
+        if eng == "pe":
+            for a in outs:
+                (wr if kw.get("grp") is not None else rd).append(("b", a[1] + "#", 0, 1, 1))
         me = len(ops)
-        deps = set(kw.get("after", []))
+        deps, raw = set(kw.get("after", [])), set(kw.get("after", []))
         for lst, w in ((rd, False), (wr, True)):
             for a in lst:
-                lo, hi = (0, 1 << 20) if a[1] in WHOLE else (a[2], a[3])
                 for (o, l2, h2, w2) in acc.get(a[1], []):
-                    if (w or w2) and l2 < hi and lo < h2:
+                    if (w or w2) and l2 < a[3] and a[2] < h2:
                         deps.add(o)
+                        if not w:
+                            raw.add(o)
         for lst, w in ((rd, False), (wr, True)):
             for a in lst:
-                lo, hi = (0, 1 << 20) if a[1] in WHOLE else (a[2], a[3])
-                acc.setdefault(a[1], []).append((me, lo, hi, w))
+                acc.setdefault(a[1], []).append((me, a[2], a[3], w))
         deps.discard(me)
         if kw.get("grp") is not None:
             deps = set(d for d in deps if ops[d].get("grp") != kw["grp"] or ops[d].get("opens"))
-        o = {"eng": eng, "ins": ins, "deps": deps, "cost": cost, "banks": set(a[1] for a in rd + wr if psum(a)),
-             "name": "%s<-%s" % (outs[0][1] if outs and outs[0][0] == "b" else "ix", ",".join(str(a[1]) for a in rd[:2]))}
+        parts = cost if isinstance(cost, list) else None
+        if parts:
+            cost = sum(PRICE[k][0] + PRICE[k][1] * n for k, n in parts)
+        o = {"on": eng, "ins": {eng: ins}, "deps": deps, "raw": raw, "cost": cost, "parts": parts, "banks": banks,
+             "name": "%s<%s" % (outs[0][1] if outs and outs[0][0] == "b" else "ix", ",".join(str(a[1]) for a in rd[:2]))}
         o.update(kw)
         ops.append(o)
         return me
 
     def vc(n, out, ins, f=1.0):
         if out[0] == "i":
-            return 0.05 + n * SCAT * CY
+            return [("s", n)]
         if ins[0][0] == "i":
-            return 0.05 + n * GA * CY
-        return 0.04 + max(64, n * f) * CY
+            return [("g", n)]
+        return [("v", max(64, n * f))]
 
     def half(*aps):
         return 0.5 if all(a[0] == "b" and wide(a) == 2 for a in aps) else 1.0
@@ -156,323 +163,330 @@ def build():
         return lambda g, T: g.vector.tensor_scalar(ap(T, out), ap(T, in0), ap(T, s1), ap(T, s2), op0, op1)
 
     def ts(out, in0, s1, s2, op0, op1=None):
-        return add(["dve"], {"dve": [i_ts(out, in0, s1, s2, op0, op1)]}, [out], [in0, s1, s2],
-                   {"dve": vc(cnt(in0), out, [in0], half(out, in0))})
+        return add("dve", [i_ts(out, in0, s1, s2, op0, op1)], [out], [in0, s1, s2], vc(cnt(in0), out, [in0], half(out, in0)))
 
     def tsm(calls):
-        return add(["dve"], {"dve": [i_ts(*c) for c in calls]}, [c[0] for c in calls], [a for c in calls for a in c[1:4]],
-                   {"dve": sum(vc(cnt(c[1]), c[0], [c[1]], half(c[0], c[1])) for c in calls)})
+        return add("dve", [i_ts(*c) for c in calls], [c[0] for c in calls], [a for c in calls for a in c[1:4]],
+                   [vc(cnt(c[1]), c[0], [c[1]], half(c[0], c[1]))[0] for c in calls])
 
     def tt(out, in0, in1, op):
         f = 1.0 if (psum(in0) or psum(in1)) else 2.0
-        return add(["dve"], {"dve": [lambda g, T: g.vector.tensor_tensor(ap(T, out), ap(T, in0), ap(T, in1), op)]}, [out], [in0, in1],
-                   {"dve": vc(cnt(in1), out, [in0], f)})
+        return add("dve", [lambda g, T: g.vector.tensor_tensor(ap(T, out), ap(T, in0), ap(T, in1), op)], [out], [in0, in1],
+                   vc(cnt(in1), out, [in0], f))
 
     def scan(out, d0, d1, op0, op1):
-        return add(["dve"], {"dve": [lambda g, T: g.vector.tensor_tensor_scan(ap(T, out), ap(T, d0), ap(T, d1), 0.0, op0, op1)]},
-                   [out], [d0, d1], {"dve": vc(cnt(d0), out, [d0], half(out, d0, d1))})
+        return add("dve", [lambda g, T: g.vector.tensor_tensor_scan(ap(T, out), ap(T, d0), ap(T, d1), 0.0, op0, op1)],
+                   [out], [d0, d1], vc(cnt(d0), out, [d0], half(out, d0, d1)))
 
     def ms(out, val):
-        return add(["dve"], {"dve": [lambda g, T: g.vector.memset(ap(T, out), val)]}, [out], [], {"dve": vc(cnt(out), out, [out], 0.5)})
+        return add("dve", [lambda g, T: g.vector.memset(ap(T, out), val)], [out], [], vc(cnt(out), out, [out], half(out)))
 
     def ac(n, in_):
-        return 0.1 + n * (GA if in_[0] == "i" else 1.0) * CY
+        return [("ag" if in_[0] == "i" else "a", n)]
 
-    def act(out, in_, func, bias=0.0, scale=1.0, accum=None):
+    def act(out, in_, func, bias=0.0, scale=1.0):
         def f(g, T):
-            if accum is not None:
-                return g.scalar.activation(ap(T, out), ap(T, in_), func, bias=ap(T, bias), scale=scale, accum_out=ap(T, accum))
             if func == AF.Copy:
                 return g.scalar.activation(ap(T, out), ap(T, in_), func, scale=scale)
             return g.scalar.activation(ap(T, out), ap(T, in_), func, bias=ap(T, bias), scale=scale)
-        return add(["act"], {"act": [f]}, [out] + ([accum] if accum else []), [in_, bias], {"act": ac(cnt(in_), in_)})
+        return add("act", [f], [out], [in_, bias], ac(cnt(in_), in_))
 
-    def cp(out, in_, engs=("dve",)):
-        n = cnt(in_)
-        return add(list(engs), {"dve": [lambda g, T: g.vector.tensor_copy(ap(T, out), ap(T, in_))],
-                                "act": [lambda g, T: g.scalar.activation(ap(T, out), ap(T, in_), AF.Copy)]},
-                   [out], [in_], {"dve": vc(n, out, [in_], half(out, in_)), "act": ac(n, in_)})
+    def cp(out, in_, who="v", scale=1.0):
+        if who == "a":
+            return act(out, in_, AF.Copy, scale=scale)
+        if scale != 1.0:
+            return ts(out, in_, scale, None, AL.mult)
+        return add("dve", [lambda g, T: g.vector.tensor_copy(ap(T, out), ap(T, in_))], [out], [in_],
+                   vc(cnt(in_), out, [in_], half(out, in_)))
 
     def mm(calls, **kw):
-        calls = [list(c) for c in calls]
+        sums = calls if isinstance(calls[0], list) else [calls]
+        calls = [list(c) + [i == 0, i == len(s) - 1] for s in sums for i, c in enumerate(s)]
+        if kw.get("grp") is not None:
+            for c in calls:
+                c[3] = c[4] = False
 
         def one(c):
             return lambda g, T: g.tensor.matmul(ap(T, c[0]), ap(T, c[1]), ap(T, c[2]), c[3], c[4])
-        cost = 0.05 + sum(max(min(64, cnt(c[1])), cnt(c[2])) * (4 if wide(c[1]) == 4 else 1) * PECY for c in calls)
-        return add(["pe"], {"pe": [one(c) for c in calls]}, [c[0] for c in calls], [a for c in calls for a in c[1:3]], {"pe": cost},
-                   calls=calls, **kw)
+        cost = [("p0", 0)] + [("p", max(min(64, cnt(c[1])), cnt(c[2])) * (4 if wide(c[1]) == 4 else 1)) for c in calls]
+        return add("pe", [one(c) for c in calls], [c[0] for c in calls], [a for c in calls for a in c[1:3]], cost, calls=calls, **kw)
 
     def iota(out, pattern, base, cm):
         def f(g, T):
             if SCRATCH[out[1]][2] == I32:
                 return g.iota(ap(T, out), pattern, base, cm)
             return g.iota(ap(T, out), pattern, base, cm, allow_small_or_imprecise_dtypes=True)
-        return add(["pool"], {"pool": [f]}, [out], [], {"pool": 0.13 + 2 * cnt(out) * CY})
+        return add("pool", [f], [out], [], 0.13 + 2 * cnt(out) * CY)
 
     def select(out, in_, pattern, cmp, fill, cm):
-        return add(["pool"], {"pool": [lambda g, T: g.affine_select(ap(T, out), ap(T, in_), pattern, cmp, fill, 0, cm)]},
-                   [out], [in_], {"pool": 0.17 + 2 * cnt(out) * CY})
+        return add("pool", [lambda g, T: g.affine_select(ap(T, out), ap(T, in_), pattern, cmp, fill, 0, cm)],
+                   [out], [in_], 0.17 + 2 * cnt(out) * CY)
 
-    def dma(q, sem, f, outs, inps, lat):
-        return add([q], {q: [f]}, outs, inps, {q: 0.1 if q != "pool" else 0.5}, sem=sem, lat=lat)
+    def dma(q, sem, f, outs, inps, lat, **kw):
+        return add(q, [f], outs, inps, 0.1 if q != "pool" else 0.5, sem=sem, lat=lat, **kw)
 
-    FLEX, ACT = ("act", "dve"), ("act",)
     ms(B("ld_v"), 0)
     ms(B("ld_j"), 0)
-    dma("sync", "l_v", lambda g, T: g.sync.dma_start(T.ld_v[0:128:16, :], T.v0[:]), [B("ld_v")], [], 2.0)
-    dma("sync", "l_x", lambda g, T: g.sync.dma_start(T.X[:, 0:NP], T.x[:]), [B("X", 0, NP)], [], 4.5)
-    dma("sync", "l_nb", lambda g, T: g.sync.dma_start(T.NB[:], T.nb[:]), [B("NB")], [], 8.0)
-    dma("act", "l_a", lambda g, T: g.scalar.dma_start(T.ld_a[:], T.a0[:]), [B("ld_a")], [], 2.5)
+    k = dma("act", "l_a", lambda g, T: g.scalar.dma_start(T.ld_a[:], T.a0[:]), [B("ld_a")], [], 2.2)
+    dma("act", "l_v", lambda g, T: g.scalar.dma_start(T.ld_v[0:128:16, :], T.v0[:]), [B("ld_v")], [], 2.2, soft=[k])
+    k = dma("sync", "l_x", lambda g, T: g.sync.dma_start(T.X[:, 0:NP], T.x[:]), [B("X", 0, NP)], [], 4.0)
+    k = dma("sync", "l_nb", lambda g, T: g.sync.dma_start(T.NB[:], T.nb[:]), [B("NB")], [], 8.0, soft=[k])
     dma("act", "l_j", lambda g, T: g.scalar.dma_start(T.ld_j[0:128:16, :], T.j0[:]), [B("ld_j")], [], 2.8)
     dma("act", "l_z", lambda g, T: g.scalar.dma_start(T.snd[:, 0:HS], T.z0[:, 0:HS]), [B("snd", 0, HS)], [], 3.2)
     dma("act", "l_z1", lambda g, T: g.scalar.dma_start(T.snd[:, PW:PW + HS], T.z0[:, HS:NS]), [B("snd", PW, PW + HS)], [], 3.4)
     dma("act", "l_y", lambda g, T: g.scalar.dma_start(T.Y[:], T.y0[:]), [B("Y")], [], 3.5)
     iota(B("ci", 0, 1), [[0, 1]], 0, 1)
     iota(B("xi"), [[1, 144]], 0, 0)
-    iota(B("xp"), [[1, 128]], 0, -1)
     iota(B("x16"), [[16, 8], [0, 16]], 0, 0)
     iota(B("xm"), [[0, 8], [1, 16]], 0, 0)
+    iota(B("xp"), [[1, 128]], 0, -1)
     dma("pool", "l_w", lambda g, T: g.dma_start(T.ld_w[:, 0:1], T.w[:], allow_slow_non_contiguous=True), [B("ld_w")], [], 3.0)
     ms(B("X", NP, XW), 0.0)
 
     def col(name, c):
         return B(name, c, c + 1)
-    G16, LC, THR, DC, C7, E1, WH, WL, W7 = (col("cf", c) for c in range(9))
+    room = {"cb": 0, "ch": 0, "c32": 0}
+
+    def new(buf, n=128):
+        room[buf] += n
+        return B(buf, room[buf] - n, room[buf])
+    turn = [0]
+
+    def times(src, c, buf="cb"):
+        out = new(buf, cnt(src))
+        cp(out, src, C["consts"][turn[0] % len(C["consts"])], c)
+        turn[0] += 1
+        return out
+    G16, LC, THR, DC, BIAS, WH, WL, W7, WC, C7, E1 = (col("cf", c) for c in range(11))
     tsm([(col("ci", 1), col("ci", 0), 112, None, AL.bitwise_and), (col("ci", 2), col("ci", 0), 15, None, AL.bitwise_and)])
     cp(B("cf", 0, 2), B("ci", 1, 3))
-    tsm([(THR, LC, 85.0, 85.0, AL.mult, AL.add), (DC, LC, float(SPARE), -2.0, AL.add, AL.mult),
+    tsm([(THR, LC, -85.0, -205.0, AL.mult, AL.add), (DC, LC, float(SPARE), -2.0, AL.add, AL.mult), (BIAS, LC, 15.0, -4096.0, AL.is_lt, AL.mult),
          (C7, LC, 160.0, 15.0, AL.mult, AL.add), (E1, LC, -144.0, 1151.0, AL.mult, AL.add)])
     ts(B("eo", 0, 1), E1, C7, 0.0, AL.min, AL.max)
-    names = ["I", "nI", "Kc", "WH", "WL", "zero", "nBu"]
-    cb = dict((n, B("cb", 128 * i, 128 * i + 128)) for i, n in enumerate(names))
-    ms(cb["zero"], 0.0)
-    mo = dict((n, 1024 + 144 * i) for i, n in enumerate(["M1", "M2", "Mn", "Ms", "Mw"]))
-    B16, B32, Bn16 = B("cb", 1744, 1752), B("cb", 1760, 1768), B("cb", 1776, 1784)
-    B1, B2, Bn1 = B("cb", 1792, 1800), B("cb", 1808, 1816), B("cb", 1824, 1832)
-    I16, Blk16, I8, TriU = (B("ch", 128 * i, 128 * i + 128) for i in range(4))
-    In4, THT = B("ch", 1168, 1296), B("tht")
-    MASK, SEG = B("ch", 512, 640), B("ch", 768, 896)
-    ONES, RST, BLK, t1, t2, t3, DUMP = (B("c32", 128 * i, min(128 * i + 128, 784)) for i in range(7))
-
-    def M(n, d):
-        if n == "h":
-            return B("ch", 1024 + 15 - d, 1024 + 143 - d)
-        return B("cb", mo[n] + 15 - d, mo[n] + 143 - d)
-
-    def MM(n):
-        return B("cb", mo[n], mo[n] + 144)
-    tsm([(B("ch", 1024, 1168), B("xi"), G16, 15.0, AL.subtract, AL.is_equal),
-         (Blk16, B("x16"), G16, None, AL.is_equal),
-         (MM("M1"), B("xi"), G16, 15.0, AL.subtract, AL.is_equal),
-         (BLK, B("x16"), G16, None, AL.is_equal),
-         (cb["I"], B("xp"), 0.0, None, AL.is_equal),
-         (cb["nI"], B("xp"), 0.0, -1.0, AL.is_equal, AL.mult),
-         (MASK, B("xm"), LC, None, AL.is_equal)])
-    act(MM("M2"), MM("M1"), AF.Copy, scale=2.0)
-    act(MM("Mn"), MM("M1"), AF.Copy, scale=-1.0)
-    act(MM("Ms"), MM("M1"), AF.Copy, scale=0.0625)
-    act(I16, cb["I"], AF.Copy)
-    act(cb["Kc"], B("xm", 0, 128), AF.Copy)
-    act(B16, B("c32", 256, 384, 16), AF.Copy, scale=16.0)
-    act(B32, B("c32", 256, 384, 16), AF.Copy, scale=32.0)
-    act(Bn16, B("c32", 256, 384, 16), AF.Copy, scale=-16.0)
-    ms(ONES, 1.0)
-    act(B1, B("c32", 256, 384, 16), AF.Copy)
-    act(B2, B("c32", 256, 384, 16), AF.Copy, scale=2.0)
-    act(Bn1, B("c32", 256, 384, 16), AF.Copy, scale=-1.0)
-    act(I8, cb["I"], AF.Copy, scale=8192.0)
-    act(In4, cb["I"], AF.Copy, scale=-4096.0)
+    Blk16, MASK, Mh, M1, I, nBlk = new("ch"), new("ch"), new("ch", 144), new("cb", 144), new("cb"), new("cb")
+    xm = B("xm")
+    ts(Blk16, B("x16"), G16, None, AL.is_equal)
+    ts(MASK, xm, LC, None, AL.is_equal)
+    ts(Mh, B("xi"), G16, 15.0, AL.subtract, AL.is_equal)
+    ts(I, B("xp"), 0.0, None, AL.is_equal)
+    nBlk4 = times(Blk16, -4096.0, "ch")
     offs = [144 * c if c < 4 else 160 * (7 - c) + 16 for c in range(8)]
     ms(B("CT"), 0.0)
     for c in range(8):
-        act(B("CT", offs[c] + 16 * c, offs[c] + 16 * c + 16), B("ch", 512, 528), AF.Copy, scale=-0.5)
+        cp(B("CT", offs[c] + 16 * c, offs[c] + 16 * c + 16), S(MASK, 0, 16), "av"[c & 1], -0.5)
     ms(B("CT", 0, TRI, 144), 4096.0)
     ms(B("CT", 16, TRI, 160), 4096.0)
-    tsm([(DUMP, B("xi", 0, 16), -32.0, DC, AL.mult, AL.add), (RST, B("xm", 0, 128), 0.0, 1000000.0, AL.is_equal, AL.mult),
-         (SEG, B("xm"), 0.0, None, AL.not_equal)])
-    act(THT, B("xm"), AF.Identity, bias=85.0, scale=85.0)
-    ts(t1, B("xm", 0, 128), float(min(UL2.values())), -1.0, AL.is_ge, AL.mult)
-    tt(cb["nBu"], t1, BLK, AL.mult)
-    act(t2, BLK, AF.Copy, scale=-4096.0)
+    DUMP = new("c32", 16)
+    ts(DUMP, B("xi", 0, 16), -32.0, DC, AL.mult, AL.add)
+    cp(nBlk, Blk16, "v", -1.0)
+    cp(M1, Mh)
+    B1, B2, Bn1 = times(S(Blk16, 0, 128, 16), 1.0), times(S(Blk16, 0, 128, 16), 2.0), S(nBlk, 0, 128, 16)
+    nI, I16, If, I4, Kc = times(I, -1.0), times(I, 1.0, "ch"), times(I, 1.0, "c32"), times(I, 4096.0), times(xm, 0.0625)
+    RST, SEG, RUN = new("c32"), new("ch"), new("cb")
+    ts(RST, xm, 0.0, 1000000.0, AL.is_equal, AL.mult)
+    M2, Mn = times(M1, 2.0), times(M1, -1.0)
+    part = {}
+
+    def nB(who):
+        if who == "vvvv":
+            return nBlk
+        if who not in part:
+            part[who] = times(nBlk, 1.0)
+            for r in range(4):
+                if who[r] == "a":
+                    ms(S(part[who], r, 128, 4), 0.0)
+        return part[who]
+    for t in range(1, RO + 1):
+        nB(C["D2"][t])
+    ts(SEG, xm, 0.0, None, AL.not_equal)
+    ts(RUN, xm, 0.0, None, AL.is_equal)
+    THn, I24, In24 = times(xm, -85.0, "ch"), times(I, 2.0 ** 24), times(I, -2.0 ** 24)
+    hI, I15, Ms = times(I, 0.5), times(I, -1.5), times(M1, 0.0625)
+    K128, ONES, K120, THu, TriU, t2, t3 = new("cb"), new("cb"), new("cb", 32), new("ch"), new("cb"), new("c32"), new("c32")
+    ms(K128, 1.0 / 128)
+    ms(ONES, 1.0)
+    ms(K120, -120.0 / 4096)
+    ms(B("cum", HS, 2 * PW, PW), 1.0)
+    ts(THu, ONES, THR, None, AL.mult)
+    cp(t2, Blk16, "a", -2.0 ** 24)
     select(t3, t2, [[-1, 128]], AL.is_gt, 0.0, 1)
-    select(TriU, t3, [[-1, 128]], AL.not_equal, 4096.0, 1)
+    select(TriU, t3, [[-1, 128]], AL.not_equal, 2.0 ** 24, 1)
     iota(B("TR"), [[1, XW + 8]], -8, 0)
-    if OPT["tr3"]:
+    if "1" in C["tr3"]:
         iota(B("T3"), [[1, XW]], 0, 0)
     tsm([(col("ci", 4), col("ld_w", 0), 4080, None, AL.bitwise_and), (col("ci", 5), col("ld_w", 0), 15, None, AL.bitwise_and),
-         (col("ci", 6), col("ld_w", 0), 127, None, AL.bitwise_and)])
-    cp(B("cf", 6, 9), B("ci", 4, 7))
-    tsm([(cb["WH"], BLK, WH, None, AL.mult), (cb["WL"], BLK, WL, None, AL.mult), (MM("Mw"), MM("M1"), W7, None, AL.mult)])
+         (col("ci", 6), col("ld_w", 0), 127, None, AL.bitwise_and), (col("ci", 7), col("ld_w", 0), 2048, None, AL.bitwise_and)])
+    cp(B("cf", 5, 9), B("ci", 4, 8))
+    ts(WC, WC, -2.0, WH, AL.mult, AL.add)
+    cWH, cWL, Mw = new("cb"), new("cb"), new("cb", 144)
+    tsm([(cWH, nBlk, WC, -1.0 / 4096, AL.mult, AL.mult), (cWL, nBlk, WL, -1.0 / 4096, AL.mult, AL.mult), (Mw, M1, W7, None, AL.mult)])
 
-    def wrap(out, m, src, n, block=False):
-        lo = src[2]
-        return mm([(out, M(m, d), B(src[1], lo + n * d, lo + n * d + n) if block else B(src[1], lo + d, src[3], 16), d == 0, d == 15)
-                   for d in range(16)])
+    def M(m, d):
+        return S(m, 15 - d, 143 - d)
+
+    def wrap(out, m, src, block=False):
+        n = cnt(out)
+        return [(out, M(m, d), S(src, n * d, n * d + n) if block else S(src, d, None, 16)) for d in range(16)]
 
     def send(t):
-        s = add(["pool"], {"pool": ["send"]}, [], [B("snd", t * PW, t * PW + PW)], {"pool": 1.0}, t=t, sem="left", lat=1.0)
+        s = add("pool", ["send"], [], [B("snd", t * PW, t * PW + PW)], 1.0, t=t, sem="left", lat=1.0)
         out = B("rcv", t * PW, t * PW + PW) if t < 2 * RO else col("home", t - 2 * RO)
-        return add(["none"], {}, [out], [], {"none": MOVE}, sem="arr%d" % t, after=[s], lat=0.0)
+        return add("none", [], [out], [], MOVE, sem="arr%d" % t, after=[s], lat=0.0)
 
-    def lowest(k, rep16, wf, wn, out, shift, na):
-        eq, sc, da, db = "eq%d" % k, "sc%d" % k, "da%d" % k, "db%d" % k
-        for c in range(8):
-            o, i = B(eq, offs[c], offs[c] + 16 * c + 16), B(rep16[1], rep16[2], rep16[2] + 16 * c + 16)
-            if c >= 8 - na:
-                act(o, i, AF.Abs, bias=B(wn[1], c, c + 1))
-            else:
-                ts(o, i, B(wf[1], c, c + 1), None, AL.not_equal)
-        scan(B(sc), B("CT"), B(eq), AL.add, AL.min)
-        tt(B(da), IX(B(sc), B("eo", 0, 1)), DUMP, AL.mult)
-        tt(B(db), B(da, 0, 8), wf, AL.max)
-        ts(out, B(db), float(shift), None, AL.add)
+    def lists(k, src, rep, wr, out, shift, keep, plain=None):
+        eq, sc, da, db = "eq%d" % k, B("sc%d" % k), B("da%d" % k), B("db%d" % k)
+        mm([wrap(wr, Mh, src), [(rep, Blk16, src)]])
+        if plain:
+            cp(plain, wr)
+        for part in ((0, 7, 1, 6), (2, 5, 3, 4)):
+            tsm([(B(eq, offs[c], offs[c] + 16 * c + 16), S(rep, 0, 16 * c + 16), S(wr, c, c + 1), None, AL.not_equal) for c in part])
+        cp(keep, rep, "a")
+        scan(sc, B("CT"), B(eq), AL.add, AL.min)
+        tt(da, IX(sc, B("eo", 0, 1)), DUMP, AL.mult)
+        tt(db, S(da, 0, 8), wr, AL.max)
+        ts(out, db, shift, None, AL.add)
+
+    def vr(t):
+        return B("vr", NU * t, NU * t + NU)
+
+    def vw(t):
+        return B("vw", 8 * t, 8 * t + 8)
+
+    def vo(t):
+        return B("vo", 8 * t, 8 * t + 8)
 
     def place_lists(t):
-        mm([(B("PN", 0, 128), Blk16, B("sel"), True, True)])
-        wrap(B("PN", 384, 392), "h", B("sel"), 8)
-        cp(B("vw", 8 * t, 8 * t + 8), B("PN", 384, 392))
-        cp(B("vf"), B("PN", 384, 392))
-        if NA[0][t]:
-            act(B("vn"), B("vf"), AF.Copy, scale=-1.0)
-        cp(B("vr", NU * t, NU * t + NU), B("PN", 0, 128), ACT)
-        lowest(0, B("vr", NU * t), B("vf"), B("vn"), B("vo", 8 * t, 8 * t + 8), 0, NA[0][t])
+        lists(0, B("sel"), B("PN", 0, 128), B("PN", 128, 136), vo(t), 0.0, vr(t), vw(t))
+
+    def rewrap(out, win, lst, m1, m2):
+        tt(m1, IX(win, lst), MASK, AL.mult)
+        scan(m2, SEG, m1, AL.mult, AL.max)
+        cp(out, S(m2, 15, None, 16))
 
     def gather(dst, lst, n, who, s0=0):
         k = n // len(who)
         for q, e in enumerate(who):
             c = s0 + q * k
-            cp(B(dst, 16 * c, 16 * (c + k)), IX(B("X", 0, NP), B(lst, c, c + k)), {"a": ACT, "v": ("dve",), "f": FLEX}[e])
+            cp(B(dst, 16 * c, 16 * (c + k)), IX(B("X", 0, NP), B(lst, c, c + k)), e)
 
     flip = [0]
 
-    def dists(src, tmp, n, opnd, opP, l0, nl, first, red, s0=0, grp=None, more=()):
-        per = 512 // n
-        steps = []
-        for c in range(0, l0, per):
-            steps.append(("a", list(range(c, min(c + per, l0)))))
-        vs = [("v", list(range(l, min(l + PAIR, nl)))) for l in range(l0, nl, PAIR)]
-        order = []
-        while steps or vs:
-            for _ in range(per // PAIR):
-                if vs:
-                    order.append(vs.pop(0))
-            if steps:
-                order.append(steps.pop(0))
-        if l0 < nl:
-            mm([(opP, cb["I"], opnd, True, True)])
-        if grp is None:
-            grp = len(ops)
-        if first:
-            mm(first, grp=grp, opens=True)
+    def dists(src, tmp, opnd, rep, who, nl, first, red, rest, s0=0):
+        base, grp = 16 * s0, len(ops)
+        mm(first, grp=grp, opens=True)
 
         def a(l):
-            return B(src, 16 * s0 + l, 16 * (s0 + n), 16)
-        for c in more:
-            mm([c + (False, False)], grp=grp)
-        for c in range(l0, nl, 4):
-            mm([x + (False, False) for l in range(c, min(c + 4, nl)) for x in red(l, "v", None, a(l))[1:]], grp=grp)
-        for i, (path, ls) in enumerate(order):
-            tile = B(tmp, 16 * s0 + ls[0] * n, 16 * s0 + (ls[-1] + 1) * n)
-            if path == "a":
+            return B(src, base + l, base + 2048, 16)
+        for r in range(4):
+            ls, lo = [l for l in range(r, nl, 4)], base + 512 * r
+            if who[r] == "v":
+                mm(rest(r) + [red(l, "v", None, a(l))[1] for l in ls], grp=grp)
+                for two in (ls[:2], ls[2:]):
+                    tiles = [(l, B(tmp, lo + 128 * (l // 4), lo + 128 * (l // 4) + 128)) for l in two]
+                    for l, tile in tiles:
+                        tt(tile, a(l), rep, AL.max)
+                    mm([red(l, "v", tile, None)[0] for l, tile in tiles], grp=grp)
+            else:
                 bank = "PD%d" % flip[0]
                 flip[0] ^= 1
-                calls = []
-                for q, l in enumerate(ls):
-                    o = B(bank, q * n, q * n + n)
-                    calls += [(o, cb["I"], a(l), True, False), (o, cb["nI"], opnd, False, True)]
-                mm(calls)
-                act(tile, B(bank, 0, len(ls) * n), AF.Abs)
-            else:
-                for l in ls:
-                    tt(B(tmp, 16 * s0 + l * n, 16 * s0 + l * n + n), a(l), opP, AL.max)
-            mm([red(l, path, B(tmp, 16 * s0 + l * n, 16 * s0 + l * n + n), a(l))[0] + (False, False) for l in ls], grp=grp)
-        return grp
+                mm([[(B(bank, 128 * q, 128 * q + 128), I, a(l)), (B(bank, 128 * q, 128 * q + 128), nI, opnd)] for q, l in enumerate(ls)])
+                act(B(tmp, lo, lo + 128 * len(ls)), B(bank, 0, 128 * len(ls)), AF.Abs)
+                mm([red(l, "a", B(tmp, lo + 128 * q, lo + 128 * q + 128), None)[0] for q, l in enumerate(ls)], grp=grp)
 
     cp(B("sel"), B("ld_v"))
     place_lists(0)
+
     def aold(t):
         return B("A", NU * (1 - (t & 1)), NU * (1 - (t & 1)) + NU)
-    act(t1, cb["I"], AF.Copy)
-    cp(aold(1), B("ld_a"))
     cp(B("A16"), B("ld_a"))
+    cp(aold(1), B("ld_a"), "v", 4096.0)
     cp(B("jh"), B("ld_j"))
-    wrap(B("PS0", 0, 16), "h", B("jh"), 16)
+    mm(wrap(B("PS0", 0, 16), Mh, B("jh")))
     for hf in range(2):
         cp(B("snd", hf * PW + HS, hf * PW + PW), B("PS0", 8 * hf, 8 * hf + 8))
         send(hf)
     for o in ops:
-        o["boost"] = EARLY[0] if o["eng"] == ["act"] or o["name"][:2] in ("TR", "T3") else EARLY[1]
+        o["boost"] = C["early"][1] if o["on"] in ("sync", "none") or "sem" in o else C["early"][0]
 
     def users_a(t):
-        vw_old, vw = B("vw", 8 * t - 8, 8 * t), B("vw", 8 * t, 8 * t + 8)
-        cp(B("n16"), IX(B("NB"), vw_old))
-        cp(B("n32"), B("n16"))
+        cp(B("n16"), IX(B("NB"), vw(t - 1)))
+        cp(B("nh"), B("n16"))
         k = len(ops)
-        gather("g2", "A16", NU, G2[t])
+        gather("g2", "A16", NU, C["G2"][t])
         for o in ops[k:]:
-            o["boost"] = EARLY[2] if t == 1 else 0.0
-        gather("g1", "n16", NU, G1[t])
+            o["boost"] = C["early"][2] if t == 1 else C["walk"][0]
+        k = len(ops)
+        gather("g1", "n16", NU, C["G1"][t])
+        for o in ops[k:]:
+            o["boost"] = C["walk"][1] if t > 1 else 0.0
+        key = B("PK", 0, 128)
 
         def red1(k, path, tile, a):
             o = B("PK", k, 128, 16)
-            if path == "a":
-                return [(o, tile, B16)]
-            return [(o, tile, B32), (o, a, Bn16), (o, B("Y"), Bn16)]
-        dists("g1", "e1", NU, B("Y"), B("PO", 256, 384), UL1[t], 16, [(B("PK", 0, 128), cb["I"], cb["Kc"], True, False)], red1)
-        scan(B("pm"), RST, B("PK", 0, 128), AL.add, AL.min)
-        if REV:
-            add(["dve"], {"dve": [lambda g, T: g.vector.tensor_tensor_scan(T.df[:, ::-1], ap(T, RST), T.pm[:, ::-1], 0.0, AL.add, AL.min)]},
-                [B("df")], [RST, B("pm")], {"dve": 0.04 + 128 * CY})
-            tt(B("eqT"), B("PK", 0, 128), B("df"), AL.is_equal)
-        else:
-            tsm([(B("eqT", 16 * q, 16 * q + 16), B("PK", 16 * q, 16 * q + 16), col("pm", 16 * q + 15), None, AL.is_equal)
-                 for q in range(8)])
-        mm([(B("PK", 128, 256), B("eqT"), cb["I"], True, True)])
-        tt(B("sel"), B("PK", 128, 256), B("n32"), AL.mult)
+            return [(o, tile, B1)] if path == "a" else [(o, tile, B2), (o, a, Bn1)]
+        if "v" in C["D1"][t]:
+            mm([(B("PO", 256, 384), I, B("Y"))])
+        dists("g1", "e1", B("Y"), B("PO", 256, 384), C["D1"][t], 16, [(key, I, Kc)], red1,
+              lambda r: [(B("PK", r, 128, 4), B("Y"), S(nBlk, r, 128, 4))])
+        scan(B("pm"), RST, key, AL.add, AL.min)
+        add("dve", [lambda g, T: g.vector.tensor_tensor_scan(T.df[:, ::-1], ap(T, RST), T.pm[:, ::-1], 0.0, AL.add, AL.min)],
+            [B("df")], [RST, B("pm")], [("v", 128)])
+        tt(B("eqT"), key, B("df"), AL.is_equal)
+        mm([(B("PK", 128, 256), B("eqT"), I4), (B("PK", 128, 256), I16, B("nh"))])
+        act(B("sel"), B("PK", 128, 256), AF.Relu, bias=-4096.0)
         place_lists(t)
-        cp(B("xn"), IX(B("X", 0, NP), vw), ACT if OPT["xn%d" % t] else ("dve",))
+        cp(B("xn"), IX(B("X", 0, NP), vw(t)), C["xn"][t])
+        who = C["D2"][t]
 
         def red2(l, path, tile, a):
             o = B("PU", 0, 128)
-            if path == "a":
-                return [(o, M("M1", l), tile)]
-            return [(o, M("M2", l), tile), (o, M("Mn", l), a)]
-        more = [(B("PU", 0, 128), cb["nBu"], B("xn"))] if UL2[t] < 16 else []
-        dists("g2", "e2", NU, B("xn"), B("PO", 384, 512), UL2[t], 16, [], red2, more=more)
-        tt(B("PK", 256, 384), B("PN", 0, 128), aold(t), AL.subtract)
-        mm([(B("PN", 128, 256), cb["I"], B("xn"), True, False), (B("PN", 128, 256), cb["I"], B("Y"), False, True),
-            (B("PN", 256, 384), cb["I"], B("xn"), True, False), (B("PN", 256, 384), cb["nI"], B("Y"), False, True)])
-        ts(B("xw"), B("PN", 128, 256), 0.5, -0.25, AL.mult, AL.add)
-        act(B("Y"), B("PN", 256, 384), AF.Abs)
+            return [(o, M(M1, l), tile)] if path == "a" else [(o, M(M2, l), tile), (o, M(Mn, l), a)]
+        if "v" in who:
+            mm([(B("PO", 384, 512), I, B("xn"))])
+        dists("g2", "e2", B("xn"), B("PO", 384, 512), who, 16, [(B("PU", 0, 128), I16, THu)], red2,
+              lambda r: [(B("PU", 0, 128), nB(who), B("xn"))] if r == who.index("v") else [])
+        mm([[(B("PK", 0, 128), I, B("xn")), (B("PK", 0, 128), I, B("Y"))], [(B("PK", 128, 256), I, B("xn")), (B("PK", 128, 256), nI, B("Y"))]])
+        ts(B("xw"), B("PK", 0, 128), 0.5, -0.25, AL.mult, AL.add)
+        act(B("Y"), B("PK", 128, 256), AF.Abs)
+        mm([(B("PK", 256, 384), If, aold(t)), (B("PK", 256, 384), nBlk4, B("sel"))])
 
     def users_b(t):
-        cp(IX(B("X"), B("vo", 8 * t, 8 * t + 8)), B("xw"))
-        ts(B("nw"), B("PU", 0, 128), THR if t == 1 else col("th", 0), None, AL.is_gt)
-        tt(B("PK", 384, 512), B("nw"), B("PK", 256, 384), AL.mult)
-        tt(B("A", NU * (t & 1), NU * (t & 1) + NU), aold(t), B("PK", 384, 512), AL.add)
-        if t > 1:
-            mm([(B("PU", 128, 256), t1, aold(t), True, False), (B("PU", 128, 256), TriU, B("nw"), False, True)])
-            ts(B("sb"), B("PU", 128, 256), -4095.0, 0.0, AL.add, AL.max)
-            mm([(B("PU", 256, 384), Blk16, B("sb"), True, True)])
-            wrap(B("PU", 384, 392), "h", B("sb"), 8)
-            cp(B("bfw"), B("PU", 384, 392))
-            if NA[1][t]:
-                act(B("bn"), B("bfw"), AF.Copy, scale=-1.0)
-            cp(B("br"), B("PU", 256, 384), ACT)
-            lowest(1, B("br"), B("bfw"), B("bn"), B("bo"), 7, NA[1][t])
-            ts(IX(B("TR"), B("bo")), B("br"), 1.0, -1.0, AL.mult, AL.add)
-        cp(IX(B("TR", 8), B("vo", 8 * t - 8, 8 * t)), B("vr", NU * t, NU * t + NU))
-        if t == 1 and OPT["tr3"]:
-            tt(B("sb"), IX(B("TR", 8, 8 + NP), B("vw", 8, 16)), MASK, AL.mult)
-            scan(B("bh"), SEG, B("sb"), AL.mult, AL.max)
-            cp(B("bo"), B("bh", 15, NU, 16))
-            cp(B("br"), IX(B("TR", 8, 8 + NP), B("bo")), ACT)
-            cp(IX(B("T3"), B("vo", 0, 8)), B("br"))
-        if t < RO:
-            cp(B("A16"), aold(t + 1))
+        TRW = B("TR", 8, 8 + NP)
+        if t == 1:
+            ts(B("nw"), B("PU", 0, 128), -120.0, None, AL.is_gt)
         else:
-            dma("sync", "s_yv", lambda g, T: g.sync.dma_start(T.yv[:], T.vr[0:128:16, NU * RO:NU * RO + NU]), [], [B("vr", NU * RO)], 2.0)
-            dma("sync", "s_ya", lambda g, T: g.sync.dma_start(T.ya[:], ap(T, aold(RO + 1))), [], [aold(RO + 1)], 2.0)
+            ts(B("nw"), B("PU", 0, 128), col("fa", 1), col("fa", 0), AL.add, AL.is_gt)
+        tt(B("dA"), B("nw"), B("PK", 256, 384), AL.mult)
+        tt(aold(t + 1), aold(t), B("dA"), AL.subtract)
+        cp(IX(B("X"), vo(t)), B("xw"))
+        cp(B("XV"), IX(B("X", 0, NP), vw(t)), C["xv"][t])
+        if t > 1:
+            mm([(B("PU", 128, 256), If, aold(t)), (B("PU", 128, 256), TriU, B("nw"))])
+            if C["sb"][t] == "a":
+                act(B("sb"), B("PU", 128, 256), AF.Relu, bias=-4095.0, scale=1.0 / 4096)
+            else:
+                ts(B("PU", 128, 256), B("PU", 128, 256), 1.0 / 4096, -4095.0, AL.mult, AL.add)
+                ts(B("sb"), B("PU", 128, 256), 0.0, None, AL.max)
+            lists(1, B("sb"), B("PU", 256, 384), B("PU", 384, 392), B("bo", 0, 8), 7.0, B("br", 0, NU))
+            ts(IX(B("TR"), B("bo", 0, 8)), B("br", 0, NU), 1.0, -1.0, AL.mult, AL.add)
+        cp(IX(B("TR", 8), vo(t - 1)), vr(t))
+        if C["tr3"][t - 1] == "1":
+            for k in range(t):
+                m1, m2, br = (B(n, NU * k, NU * k + NU) for n in ("t1", "t2", "br"))
+                l1, l2 = B("bo", 8 + 16 * k, 16 + 16 * k), B("bo", 16 + 16 * k, 24 + 16 * k)
+                if k == t - 1:
+                    l1 = vw(t)
+                else:
+                    rewrap(l1, TRW, vw(k), m1, m2)
+                rewrap(l2, TRW, l1, m1, m2)
+                cp(br, IX(TRW, l2), "a")
+                cp(IX(B("T3"), vo(k)), br)
+        if t < RO:
+            cp(B("A16"), aold(t + 1), "v", 1.0 / 4096)
+        else:
+            cp(B("df"), aold(RO + 1), "a", 1.0 / 4096)
+            dma("sync", "s_yv", lambda g, T: g.sync.dma_start(T.yv[:], T.vr[0:128:16, NU * RO:NU * RO + NU]), [], [vr(RO)], 2.0)
+            dma("sync", "s_ya", lambda g, T: g.sync.dma_start(T.ya[:], T.df[:]), [], [B("df")], 2.0)
             dma("sync", "s_yy", lambda g, T: g.sync.dma_start(T.yy[:], T.Y[:]), [], [B("Y")], 2.0)
             dma("sync", "s_yt", lambda g, T: g.sync.dma_start(T.yt[:], T.TR[0:128:16, 8:8 + NP]), [], [B("TR")], 2.5)
 
@@ -486,83 +500,86 @@ def build():
         def H(name):
             return B(name, lo, hi)
 
+        def P(name):
+            return B(name, PW * hf, PW * hf + PW)
+
         def W(name):
             return B(name, c8, c8 + 8)
-        pu, pt, pz = B(bank, 0, HS), B(bank, HS, 2 * HS), B("PO", lo, hi)
-        cp(W("j16"), jw)
-        mm([(pu, cb["WH"], z, True, False), (pu, cb["WL"], z, False, True)])
-        cp(H("Bh"), IX(aold(t + 1), W("j16")), ACT)
-        cp(H("u1"), pu)
-        ts(H("u2"), H("u1"), 4095, None, AL.bitwise_and)
-        ts(pu, H("u2"), 32.0, None, AL.add)
-        tt(H("u2"), H("Bh"), pu, AL.mult)
+        j16, pz = W("j16"), B("PO", lo, hi)
+        p0, p1, p2, p3 = B(bank, 0, HS), B(bank, HS, 2 * HS), B(bank, 2 * HS, 3 * HS), B(bank, 3 * HS, 4 * HS)
+        cp(j16, jw)
+        mm([(p0, I, K128), (p0, cWH, z), (p0, cWL, z)])
+        ts(H("q"), p0, -2079.5 / 4096, None, AL.add)
+        tt(p1, H("q"), p0, AL.subtract)
+        if C["Bh"][t][hf] == "e":
+            cp(H("Aj"), IX(aold(t), j16), "a")
+            tt(H("Bh"), IX(B("dA"), j16), H("Aj"), AL.subtract)
+        else:
+            cp(H("Bh"), IX(aold(t + 1), j16), C["Bh"][t][hf], -1.0)
+        tt(H("u2"), H("Bh"), p1, AL.mult)
         ts(H("u1"), H("u2"), 5, 2047, AL.arith_shift_right, AL.bitwise_and)
         cp(H("h16"), H("u1"))
-        gather("g3", "h16", HS, G3[t][4 * hf:4 * hf + 4], lo)
-        cp(H("vj"), IX(B("vr", NU * t, NU * t + NU), W("j16")), ACT)
-        wrap(B("PN", 432 + c8, 440 + c8), "Mw", z, 8, last)
-        cp(W("w1"), B("PN", 432 + c8, 440 + c8))
+        gather("g3", "h16", HS, C["G3"][t][4 * hf:4 * hf + 4], lo)
+        cp(H("vj"), IX(vr(t), j16), C["vj"][t][hf])
+        mm([(pz, I, z)])
+        cp(H("xj"), IX(B("XV"), j16), C["xj"][t][hf])
+        mm([(p0, hI, H("xj")), (p0, I15, z)])
+        ts(H("q"), p0, 0.25, None, AL.add)
+        mm(wrap(S(p3, 0, 8), Mw, z, last))
+        cp(W("w1"), S(p3, 0, 8))
         ts(W("w2"), W("w1"), 127, None, AL.bitwise_and)
         if last:
-            cp(H("jr"), IX(B("xi", 0, 128), W("j16")), ACT)
-            wrap(B("PN", 448 + c8, 456 + c8), "Ms", H("jr"), 8, True)
-            cp(W("jb"), B("PN", 448 + c8, 456 + c8))
+            cp(H("jr"), IX(B("xi", 0, 128), j16), "a")
+            mm(wrap(S(p3, 8, 16), Ms, H("jr"), True))
+            cp(W("jb"), S(p3, 8, 16))
             jw = W("jb")
         tt(W("dw"), W("w2"), jw, AL.subtract)
 
         def red(l, path, tile, a):
-            o = B(bank, l, HS, 16)
-            if path == "a":
-                return [(o, tile, B1)]
-            return [(o, tile, B2), (o, a, Bn1), (o, z, Bn1)]
-        dists("g3", "e3", HS, z, pz, SL0[t][hf], 15, [(pu, cb["zero"], z, True, False)], red, lo)
-        tt(H("hit"), pu, THT, AL.is_le)
-        scan(H("cum"), SEG, H("hit"), AL.mult, AL.add)
-        mm([(pt, I16, H("Bh"), True, False), (pt, H("hit"), I8, False, False), (pt, H("cum"), In4, False, True)])
-        if RELU == "a":
-            act(H("ss"), pt, AF.Relu, bias=-4096.0)
-        else:
-            ts(H("ss"), pt, -4096.0, 0.0, AL.add, AL.max)
-        wrap(B(bank, 256, 264), "h", H("ss"), 8)
+            o = S(p2, l + 1, HS, 16)
+            return [(o, tile, B1)] if path == "a" else [(o, tile, B2), (o, a, Bn1)]
+        dists("g3", "e3", z, pz, C["D3"][t][4 * hf:4 * hf + 4], 15, [(p2, I16, THn)], red,
+              lambda r: [(S(p2, (r + 1) % 4, HS, 4), z, S(nBlk, (r + 1) % 4, 128, 4))], lo)
+        cum = P("cum")
+        grp = len(ops)
+        mm([(p1, If, H("Bh"))], grp=grp, opens=True)
+        scan(S(cum, 0, HS), p2, RUN, AL.min, AL.max)
+        mm([(p1, S(cum, 0, HS), In24), (p1, S(cum, 1, HS + 1), I24)], grp=grp)
+        act(H("ss"), p1, AF.Relu, bias=BIAS, scale=-1.0 / 4096)
+        mm(wrap(S(p3, 16, 24), Mh, H("ss")))
         c0 = 0
-        if t == 1 and OPT["tr3"]:
+        if C["tr3"][t - 1] == "1":
             c0, TRW = 2, B("T3", 0, NP)
 
         def pw(c):
             return B("pw", 32 * hf + 8 * c, 32 * hf + 8 * c + 8)
-        cp(pw(c0), B(bank, 256, 264))
+        cp(pw(c0), S(p3, 16, 24))
+        fd = H("fd")
         for c in range(c0, 3):
-            tt(H("m1"), IX(TRW, pw(c)), MASK, AL.mult)
             if c == 2:
-                tt(H("fd"), IX(TRW, pw(c)), H("vj"), AL.is_equal)
-            scan(H("m2"), SEG, H("m1"), AL.mult, AL.max)
-            cp(pw(c + 1), B("m2", lo + 15, hi, 16))
-        act(pt, H("fd"), AF.Identity, bias=1.0, scale=-2.0)
-        act(H("scl"), H("fd"), AF.Identity, bias=1.0, scale=-HALF, accum=None if last else col("fa", hf))
-        tt(H("zz"), pt, z, AL.mult)
+                tt(fd, IX(TRW, pw(c)), H("vj"), AL.is_equal)
+            rewrap(pw(c + 1), TRW, pw(c), H("m1"), H("m2"))
+        if not last:
+            o = B("PN", 400 + 32 * hf, 432 + 32 * hf)
+            mm([(o, ONES, S(fd, 32 * q, 32 * q + 32)) for q in range(4)] + ([] if hf else [(o, ONES, K120)]))
+        tt(H("fe"), fd, H("q"), AL.mult)
+        tt(H("zz"), H("fe"), pz, AL.add)
         tt(H("tz"), IX(XS, pw(3)), H("zz"), AL.subtract)
-        act(pu, H("tz"), AF.Abs)
-        tt(H("zi"), pu, H("scl"), AL.mult)
-        cp(B("snd", s0, s0 + HS), H("zi"))
-        wrap(B(bank, 272, 280), "Ms", H("fd"), 8, last)
-        tt(W("tw"), B(bank, 272, 280), W("dw"), AL.mult)
+        act(B("snd", s0, s0 + HS), H("tz"), AF.Abs)
+        mm(wrap(S(p3, 24, 32), Ms, fd, last))
+        tt(W("tw"), S(p3, 24, 32), W("dw"), AL.mult)
         tt(B("snd", s0 + HS, s0 + PW), W("tw"), jw, AL.add)
         send(2 * t + hf)
 
     def finds():
-        o = B("PN", 464, 465)
-        mm([(o, ONES, col("fa", 0), True, False), (o, ONES, col("fa", 1), False, True)])
-        ts(col("fi", 0), o, -1.0 / HALF, 32768.0 / HALF, AL.mult, AL.add)
-        ts(col("fi", 1), col("fi", 0), 255, None, AL.bitwise_and)
-        ts(col("th", 0), col("fi", 1), THR, None, AL.add)
+        add("dve", [lambda g, T: g.vector.tensor_reduce(T.fa[:, 0:1], T.PN[:, 400:464], AxisListType.X, AL.add)],
+            [col("fa", 0)], [B("PN", 400, 464)], [("v", 64)])
+        ts(col("fa", 1), col("fa", 0), 1.5 * 2.0 ** 31, 1.5 * 2.0 ** 31, AL.add, AL.subtract)
 
     users_a(1)
     users_b(1)
     for t in range(1, RO + 1):
-        k = len(ops)
         seekers(t, 0)
-        for o in ops[k:]:
-            o["boost"] = URGE
         seekers(t, 1)
         if t < RO:
             finds()
@@ -578,24 +595,29 @@ def build():
     return ops
 
 
-HALF = 0.5 + 2.0 ** -11
+def unordered(ops, d, i):
+    e = ops[i]["on"]
+    return e == ops[d]["on"] and (e == "pe" or (CFG["free"] and e in ("dve", "act") and d not in ops[i]["raw"] and "sem" not in ops[d]))
 
 
 def schedule(ops):
     n = len(ops)
-    succ = [[] for _ in ops]
-    for i, o in enumerate(ops):
-        for d in set(o["deps"]) | set(o.get("soft", [])):
-            succ[d].append(i)
-
     pred = [sorted(set(o["deps"]) | set(o.get("soft", []))) for o in ops]
-    free_of = set((d, i) for i, o in enumerate(ops) for d in o.get("soft", []) if d not in o["deps"])
-    eng = [o["eng"][0] for o in ops]
-    cost = [o["cost"][e] for o, e in zip(ops, eng)]
+    eng = [o["on"] for o in ops]
+    cost = [o["cost"] for o in ops]
     lat = [o.get("lat", 0.0) for o in ops]
+    succ = [[] for _ in ops]
+    gap = {}
+    for i, o in enumerate(ops):
+        for d in pred[i]:
+            if d not in o["deps"]:
+                gap[d, i] = -lat[d]
+            else:
+                gap[d, i] = 0.0 if unordered(ops, d, i) else (LAT0 if eng[d] == eng[i] else LAT1)
+            succ[d].append((i, gap[d, i]))
 
-    def sweep(before, after, prio, back):
-        left = [len(b) for b in before]
+    def sweep(prio):
+        left = [len(b) for b in pred]
         can = [0.0] * n
         ready = [i for i in range(n) if left[i] == 0]
         busy, done, at = {}, [0.0] * n, [0.0] * n
@@ -604,20 +626,20 @@ def schedule(ops):
             e, st = eng[i], can[i]
             held = [x for x in busy.get(e, []) if x[1] > st]
             for b in ops[i]["banks"]:
-                held += [(x[0] - LAT, x[1] + LAT) for x in busy.get(b, []) if x[2] != e and x[1] + LAT > st]
+                held += [(x[0] - LAT1, x[1] + LAT1) for x in busy.get(b, []) if x[2] != e and x[1] + LAT1 > st]
             for x in sorted(held):
                 if x[0] >= st + cost[i] - 1e-9:
                     break
                 st = max(st, x[1])
             at[i] = st
-            done[i] = st + cost[i] + (0.0 if back else lat[i])
+            done[i] = st + cost[i] + lat[i]
             if e != "none":
                 busy.setdefault(e, []).append((st, st + cost[i]))
             for b in ops[i]["banks"]:
                 busy.setdefault(b, []).append((st, st + cost[i], e))
             ready.remove(i)
-            for s in after[i]:
-                can[s] = max(can[s], done[i] + (0.0 if (e == "pe" and eng[s] == "pe") or (i, s) in free_of else LAT))
+            for s, w in succ[i]:
+                can[s] = max(can[s], done[i] + w)
                 left[s] -= 1
                 if left[s] == 0:
                     ready.append(s)
@@ -631,12 +653,15 @@ def schedule(ops):
         return max(done), order, at, extra, done
 
     prio = [0.0] * n
-    for i in reversed(sweep(pred, succ, prio, False)[1]):
-        prio[i] = cost[i] + lat[i] + LAT + max([prio[s] for s in succ[i]] + [0.0])
-    rng = np.random.default_rng(SEED)
+    for i in reversed(range(n)):
+        prio[i] = cost[i] + lat[i] + max([prio[s] + w for s, w in succ[i]] + [0.0])
+    rng = np.random.default_rng(CFG["seed"])
     prio = [p + o.get("boost", 0.0) for p, o in zip(prio, ops)]
-    best = now = sweep(pred, succ, prio, False)
-    for turn in range(TURNS):
+    for i in reversed(range(n)):
+        prio[i] = max([prio[i]] + [prio[s] + 0.01 for s, w in succ[i]])
+    best = now = sweep(prio)
+    turns = CFG["turns"]
+    for turn in range(turns):
         _, order, at, extra, done = now
         last, prev = {}, {}
         for i in order:
@@ -645,11 +670,11 @@ def schedule(ops):
         held = dict(extra)
         i, jams = max(range(n), key=lambda x: done[x]), []
         while True:
-            d = max(pred[i], key=lambda x: done[x]) if pred[i] else None
-            t = done[d] + (0.0 if eng[i] == "pe" and eng[d] == "pe" else LAT) if d is not None else 0.0
+            d = max(pred[i], key=lambda x: done[x] + gap[x, i]) if pred[i] else None
+            t = done[d] + gap[d, i] if d is not None else 0.0
             if t < at[i] - 1e-6:
                 j = prev[i]
-                if i in held and (j is None or done[held[i]] + LAT > at[j] + cost[j]):
+                if i in held and (j is None or done[held[i]] + LAT1 > at[j] + cost[j]):
                     j = held[i]
                 if j is not None:
                     jams.append((i, j))
@@ -669,13 +694,13 @@ def schedule(ops):
                     if p2[x] < top:
                         p2[x] = top
                         todo.extend(pred[x])
-        new = sweep(pred, succ, p2, False)
-        if new[0] <= now[0] + TILT * (1.0 - turn / TURNS) * float(rng.random()):
+        new = sweep(p2)
+        if new[0] <= now[0] + CFG["tilt"] * (1.0 - turn / turns) * float(rng.random()):
             now, prio = new, p2
             if new[0] < best[0]:
                 best = new
     for i, o in enumerate(ops):
-        o["on"], o["at"] = eng[i], best[2][i]
+        o["at"] = best[2][i]
     for i, d in best[3]:
         ops[i]["deps"].add(d)
     return best[1], best[0]
@@ -747,7 +772,7 @@ def rank_program(g, core, T, topo):
             continue
         need = {}
         for d in o["deps"]:
-            if e == "pe" and ops[d]["on"] == "pe":
+            if unordered(ops, d, i):
                 continue
             s, c = token[d]
             if c > need.get(s, (0, 0))[0]:

import numpy as np
from concourse.mybir import AluOpType, ActivationFunctionType, AxisListType

AL = AluOpType
AF = ActivationFunctionType
NP, NU, NS, RO = 2048, 128, 256, 3
XW = 2192
TRI = 576
HS = NS // 2
PW = HS + 8
MOVES = 2 * (RO + 1)
SPARE = 2056
F32, BF, F16, I32, U16 = "float32", "bfloat16", "float16", "int32", "uint16"

SCRATCH = {
    "X": ("sbuf", [128, XW], BF), "NB": ("sbuf", [128, NP], I32), "TR": ("sbuf", [128, XW + 8], F32),
    "ld_v": ("sbuf", [128, NU], I32), "ld_j": ("sbuf", [128, NS], I32), "ld_a": ("sbuf", [128, NU], I32),
    "ld_w": ("sbuf", [128, 4], I32), "jh": ("sbuf", [128, NS], F16),
    "Y": ("sbuf", [128, NU], BF), "A": ("sbuf", [128, 2 * NU], F32), "A16": ("sbuf", [128, NU], U16), "T3": ("sbuf", [128, XW], F32),
    "snd": ("sbuf", [128, MOVES * PW], BF), "rcv": ("sbuf", [128, (MOVES - 2) * PW], BF),
    "hop": ("dram", [MOVES, 128, PW], BF), "home": ("dram", [2, 128, PW], BF),
    "xi": ("sbuf", [128, 144], F32), "xp": ("sbuf", [128, 128], F32), "x16": ("sbuf", [128, 128], F32), "xm": ("sbuf", [128, 128], F32),
    "ci": ("sbuf", [128, 16], I32), "cf": ("sbuf", [128, 16], F32),
    "cb": ("sbuf", [128, 3600], BF), "ch": ("sbuf", [128, 1800], F16), "c32": ("sbuf", [128, 640], F32),
    "n16": ("sbuf", [128, NU], U16), "nh": ("sbuf", [128, NU], F16),
    "g1": ("sbuf", [128, NP], BF), "g2": ("sbuf", [128, NP], BF), "e1": ("sbuf", [128, NP], BF), "e2": ("sbuf", [128, NP], BF),
    "pm": ("sbuf", [128, NU], F32), "eqT": ("sbuf", [128, NU], BF), "sel": ("sbuf", [128, NU], F16),
    "vr": ("sbuf", [128, 4 * NU], F32), "vw": ("sbuf", [128, 32], U16),
    "vo": ("sbuf", [128, 32], U16), "xn": ("sbuf", [128, NU], BF), "xw": ("sbuf", [128, NU], I32), "XV": ("sbuf", [128, NU], BF),
    "df": ("sbuf", [128, NU], F32), "nw": ("sbuf", [128, NU], BF), "dA": ("sbuf", [128, NU], F32),
    "sb": ("sbuf", [128, NU], F16), "br": ("sbuf", [128, 3 * NU], F32), "bo": ("sbuf", [128, 56], U16),
    "t1": ("sbuf", [128, 3 * NU], F16), "t2": ("sbuf", [128, 3 * NU], F16), "CT": ("sbuf", [128, TRI], BF), "eo": ("sbuf", [128, 2], U16),
    "eq0": ("sbuf", [128, TRI], BF), "sc0": ("sbuf", [128, TRI], BF), "da0": ("sbuf", [128, 16], F32), "db0": ("sbuf", [128, 8], F32),
    "eq1": ("sbuf", [128, TRI], BF), "sc1": ("sbuf", [128, TRI], BF), "da1": ("sbuf", [128, 16], F32), "db1": ("sbuf", [128, 8], F32),
    "j16": ("sbuf", [128, 16], U16), "q": ("sbuf", [128, NS], I32), "u1": ("sbuf", [128, NS], I32), "u2": ("sbuf", [128, NS], I32),
    "h16": ("sbuf", [128, NS], U16), "Bh": ("sbuf", [128, NS], F32), "Aj": ("sbuf", [128, NS], F32), "vj": ("sbuf", [128, NS], F16),
    "g3": ("sbuf", [128, 2 * NP], BF), "e3": ("sbuf", [128, 2 * NP], BF),
    "cum": ("sbuf", [128, 2 * PW], BF), "ss": ("sbuf", [128, NS], F16), "pw": ("sbuf", [128, 64], U16),
    "m1": ("sbuf", [128, NS], F16), "m2": ("sbuf", [128, NS], F16), "fd": ("sbuf", [128, NS], BF),
    "xj": ("sbuf", [128, NS], BF), "fe": ("sbuf", [128, NS], F16), "zz": ("sbuf", [128, NS], BF), "tz": ("sbuf", [128, NS], BF),
    "w1": ("sbuf", [128, 16], I32), "w2": ("sbuf", [128, 16], I32), "dw": ("sbuf", [128, 16], F32), "tw": ("sbuf", [128, 16], F32),
    "jr": ("sbuf", [128, NS], BF), "jb": ("sbuf", [128, 16], F32), "fa": ("sbuf", [128, 4], F32),
    "PD0": ("psum", [128, 512], F32), "PD1": ("psum", [128, 512], F32), "PO": ("psum", [128, 512], F32), "PS0": ("psum", [128, 512], F32),
    "PK": ("psum", [128, 512], F32), "PU": ("psum", [128, 512], F32), "PS1": ("psum", [128, 512], F32), "PN": ("psum", [128, 512], F32),
}
LOADS = ["v", "x", "nb", "a", "y", "j", "z", "z1", "w"]
STORES = ["yv", "ya", "yy", "yt", "yz0", "yz1", "yj0", "yj1"]
SEMAPHORES = (["dve", "act", "pe", "pool", "left"] + ["l_" + n for n in LOADS] + ["s_" + n for n in STORES]
              + ["arr%d" % t for t in range(MOVES)] + ["rel%d" % t for t in range(MOVES)])

CFG = {
    "G1": {1: "avva", 2: "aaaa", 3: "aaaa"}, "G2": {1: "aaaa", 2: "aaaa", 3: "aaaa"},
    "G3": {1: "avaaaava", 2: "avaaaava", 3: "avavavav"},
    "D1": {1: "vavv", 2: "vvav", 3: "aaaa"}, "D2": {1: "vava", 2: "vvaa", 3: "vvva"},
    "D3": {1: "vvaavvva", 2: "vvvavvva", 3: "vaaavvaa"},
    "xn": {1: "v", 2: "v", 3: "a"}, "Bh": {1: "aa", 2: "aa", 3: "aa"}, "vj": {1: "aa", 2: "aa", 3: "aa"},
    "xv": {1: "a", 2: "a", 3: "a"}, "xj": {1: "aa", 2: "aa", 3: "aa"}, "sb": {1: "a", 2: "a", 3: "a"},
    "walk": (0.0, 6.0), "tr3": "100", "early": (0.0, 100.0, 100.0), "consts": "avva", "free": 0,
    "seed": 3, "tilt": 0.15, "turns": 2500,
}
CY, LAT0, LAT1, MOVE = 0.00086, 0.18, 0.18, 2.0
PRICE = {"v": (0.01, CY), "g": (0.05, 1.56 * CY), "s": (0.05, 3.8 * CY), "a": (0.06, CY), "ag": (0.065, 1.56 * CY),
         "p0": (0.02, 0.0), "p": (0.0, 0.5 * CY)}


def B(name, lo=0, hi=None, step=1):
    return ("b", name, lo, SCRATCH[name][1][-1] if hi is None else hi, step)


def IX(win, off):
    return ("i", win, off)


def S(a, lo, hi=None, step=1):
    return B(a[1], a[2] + lo, a[3] if hi is None else a[2] + hi, step)


def cnt(a):
    if a[0] == "i":
        return 16 * (a[2][3] - a[2][2])
    return (a[3] - a[2] + a[4] - 1) // a[4]


def isap(a):
    return isinstance(a, tuple)


def ap(T, a):
    if not isap(a):
        return a
    if a[0] == "i":
        return ap(T, a[1]).indirect(ap(T, a[2]))
    if a[4] == 1:
        return T[a[1]][:, a[2]:a[3]]
    return T[a[1]][:, a[2]:a[3]:a[4]]


def wide(a):
    return 2 if SCRATCH[a[1]][2] in (BF, F16, U16) else 4


def psum(a):
    return a[0] == "b" and SCRATCH[a[1]][0] == "psum"


def build():
    ops = []
    acc = {}
    C = CFG

    def add(eng, ins, outs, inps, cost, **kw):
        rd, wr = [], []
        for a in inps:
            if isap(a):
                rd.extend([a[1], a[2]] if a[0] == "i" else [a])
        for a in outs:
            if a[0] == "i":
                wr.append(a[1])
                rd.append(a[2])
            else:
                wr.append(a)
        banks = set(a[1] for a in rd + wr if psum(a))
        if eng == "pe":
            for a in outs:
                (wr if kw.get("grp") is not None else rd).append(("b", a[1] + "#", 0, 1, 1))
        me = len(ops)
        deps, raw = set(kw.get("after", [])), set(kw.get("after", []))
        for lst, w in ((rd, False), (wr, True)):
            for a in lst:
                for (o, l2, h2, w2) in acc.get(a[1], []):
                    if (w or w2) and l2 < a[3] and a[2] < h2:
                        deps.add(o)
                        if not w:
                            raw.add(o)
        for lst, w in ((rd, False), (wr, True)):
            for a in lst:
                acc.setdefault(a[1], []).append((me, a[2], a[3], w))
        deps.discard(me)
        if kw.get("grp") is not None:
            deps = set(d for d in deps if ops[d].get("grp") != kw["grp"] or ops[d].get("opens"))
        parts = cost if isinstance(cost, list) else None
        if parts:
            cost = sum(PRICE[k][0] + PRICE[k][1] * n for k, n in parts)
        o = {"on": eng, "ins": {eng: ins}, "deps": deps, "raw": raw, "cost": cost, "parts": parts, "banks": banks,
             "name": "%s<%s" % (outs[0][1] if outs and outs[0][0] == "b" else "ix", ",".join(str(a[1]) for a in rd[:2]))}
        o.update(kw)
        ops.append(o)
        return me

    def vc(n, out, ins, f=1.0):
        if out[0] == "i":
            return [("s", n)]
        if ins[0][0] == "i":
            return [("g", n)]
        return [("v", max(64, n * f))]

    def half(*aps):
        return 0.5 if all(a[0] == "b" and wide(a) == 2 for a in aps) else 1.0

    def i_ts(out, in0, s1, s2, op0, op1=None):
        if op1 is None:
            return lambda g, T: g.vector.tensor_scalar(ap(T, out), ap(T, in0), ap(T, s1), None, op0)
        return lambda g, T: g.vector.tensor_scalar(ap(T, out), ap(T, in0), ap(T, s1), ap(T, s2), op0, op1)

    def ts(out, in0, s1, s2, op0, op1=None):
        return add("dve", [i_ts(out, in0, s1, s2, op0, op1)], [out], [in0, s1, s2], vc(cnt(in0), out, [in0], half(out, in0)))

    def tsm(calls):
        return add("dve", [i_ts(*c) for c in calls], [c[0] for c in calls], [a for c in calls for a in c[1:4]],
                   [vc(cnt(c[1]), c[0], [c[1]], half(c[0], c[1]))[0] for c in calls])

    def tt(out, in0, in1, op):
        f = 1.0 if (psum(in0) or psum(in1)) else 2.0
        return add("dve", [lambda g, T: g.vector.tensor_tensor(ap(T, out), ap(T, in0), ap(T, in1), op)], [out], [in0, in1],
                   vc(cnt(in1), out, [in0], f))

    def scan(out, d0, d1, op0, op1):
        return add("dve", [lambda g, T: g.vector.tensor_tensor_scan(ap(T, out), ap(T, d0), ap(T, d1), 0.0, op0, op1)],
                   [out], [d0, d1], vc(cnt(d0), out, [d0], half(out, d0, d1)))

    def ms(out, val):
        return add("dve", [lambda g, T: g.vector.memset(ap(T, out), val)], [out], [], vc(cnt(out), out, [out], half(out)))

    def ac(n, in_):
        return [("ag" if in_[0] == "i" else "a", n)]

    def act(out, in_, func, bias=0.0, scale=1.0):
        def f(g, T):
            if func == AF.Copy:
                return g.scalar.activation(ap(T, out), ap(T, in_), func, scale=scale)
            return g.scalar.activation(ap(T, out), ap(T, in_), func, bias=ap(T, bias), scale=scale)
        return add("act", [f], [out], [in_, bias], ac(cnt(in_), in_))

    def cp(out, in_, who="v", scale=1.0):
        if who == "a":
            return act(out, in_, AF.Copy, scale=scale)
        if scale != 1.0:
            return ts(out, in_, scale, None, AL.mult)
        return add("dve", [lambda g, T: g.vector.tensor_copy(ap(T, out), ap(T, in_))], [out], [in_],
                   vc(cnt(in_), out, [in_], half(out, in_)))

    def mm(calls, **kw):
        sums = calls if isinstance(calls[0], list) else [calls]
        calls = [list(c) + [i == 0, i == len(s) - 1] for s in sums for i, c in enumerate(s)]
        if kw.get("grp") is not None:
            for c in calls:
                c[3] = c[4] = False

        def one(c):
            return lambda g, T: g.tensor.matmul(ap(T, c[0]), ap(T, c[1]), ap(T, c[2]), c[3], c[4])
        cost = [("p0", 0)] + [("p", max(min(64, cnt(c[1])), cnt(c[2])) * (4 if wide(c[1]) == 4 else 1)) for c in calls]
        return add("pe", [one(c) for c in calls], [c[0] for c in calls], [a for c in calls for a in c[1:3]], cost, calls=calls, **kw)

    def iota(out, pattern, base, cm):
        def f(g, T):
            if SCRATCH[out[1]][2] == I32:
                return g.iota(ap(T, out), pattern, base, cm)
            return g.iota(ap(T, out), pattern, base, cm, allow_small_or_imprecise_dtypes=True)
        return add("pool", [f], [out], [], 0.13 + 2 * cnt(out) * CY)

    def select(out, in_, pattern, cmp, fill, cm):
        return add("pool", [lambda g, T: g.affine_select(ap(T, out), ap(T, in_), pattern, cmp, fill, 0, cm)],
                   [out], [in_], 0.17 + 2 * cnt(out) * CY)

    def dma(q, sem, f, outs, inps, lat, **kw):
        return add(q, [f], outs, inps, 0.1 if q != "pool" else 0.5, sem=sem, lat=lat, **kw)

    ms(B("ld_v"), 0)
    ms(B("ld_j"), 0)
    k = dma("act", "l_a", lambda g, T: g.scalar.dma_start(T.ld_a[:], T.a0[:]), [B("ld_a")], [], 2.2)
    dma("act", "l_v", lambda g, T: g.scalar.dma_start(T.ld_v[0:128:16, :], T.v0[:]), [B("ld_v")], [], 2.2, soft=[k])
    k = dma("sync", "l_x", lambda g, T: g.sync.dma_start(T.X[:, 0:NP], T.x[:]), [B("X", 0, NP)], [], 4.0)
    k = dma("sync", "l_nb", lambda g, T: g.sync.dma_start(T.NB[:], T.nb[:]), [B("NB")], [], 8.0, soft=[k])
    dma("act", "l_j", lambda g, T: g.scalar.dma_start(T.ld_j[0:128:16, :], T.j0[:]), [B("ld_j")], [], 2.8)
    dma("act", "l_z", lambda g, T: g.scalar.dma_start(T.snd[:, 0:HS], T.z0[:, 0:HS]), [B("snd", 0, HS)], [], 3.2)
    dma("act", "l_z1", lambda g, T: g.scalar.dma_start(T.snd[:, PW:PW + HS], T.z0[:, HS:NS]), [B("snd", PW, PW + HS)], [], 3.4)
    dma("act", "l_y", lambda g, T: g.scalar.dma_start(T.Y[:], T.y0[:]), [B("Y")], [], 3.5)
    iota(B("ci", 0, 1), [[0, 1]], 0, 1)
    iota(B("xi"), [[1, 144]], 0, 0)
    iota(B("x16"), [[16, 8], [0, 16]], 0, 0)
    iota(B("xm"), [[0, 8], [1, 16]], 0, 0)
    iota(B("xp"), [[1, 128]], 0, -1)
    dma("pool", "l_w", lambda g, T: g.dma_start(T.ld_w[:, 0:1], T.w[:], allow_slow_non_contiguous=True), [B("ld_w")], [], 3.0)
    ms(B("X", NP, XW), 0.0)

    def col(name, c):
        return B(name, c, c + 1)
    room = {"cb": 0, "ch": 0, "c32": 0}

    def new(buf, n=128):
        room[buf] += n
        return B(buf, room[buf] - n, room[buf])
    turn = [0]

    def times(src, c, buf="cb"):
        out = new(buf, cnt(src))
        cp(out, src, C["consts"][turn[0] % len(C["consts"])], c)
        turn[0] += 1
        return out
    G16, LC, THR, DC, BIAS, WH, WL, W7, WC, C7, E1 = (col("cf", c) for c in range(11))
    tsm([(col("ci", 1), col("ci", 0), 112, None, AL.bitwise_and), (col("ci", 2), col("ci", 0), 15, None, AL.bitwise_and)])
    cp(B("cf", 0, 2), B("ci", 1, 3))
    tsm([(THR, LC, -85.0, -205.0, AL.mult, AL.add), (DC, LC, float(SPARE), -2.0, AL.add, AL.mult), (BIAS, LC, 15.0, -4096.0, AL.is_lt, AL.mult),
         (C7, LC, 160.0, 15.0, AL.mult, AL.add), (E1, LC, -144.0, 1151.0, AL.mult, AL.add)])
    ts(B("eo", 0, 1), E1, C7, 0.0, AL.min, AL.max)
    Blk16, MASK, Mh, M1, I, nBlk = new("ch"), new("ch"), new("ch", 144), new("cb", 144), new("cb"), new("cb")
    xm = B("xm")
    ts(Blk16, B("x16"), G16, None, AL.is_equal)
    ts(MASK, xm, LC, None, AL.is_equal)
    ts(Mh, B("xi"), G16, 15.0, AL.subtract, AL.is_equal)
    ts(I, B("xp"), 0.0, None, AL.is_equal)
    nBlk4 = times(Blk16, -4096.0, "ch")
    offs = [144 * c if c < 4 else 160 * (7 - c) + 16 for c in range(8)]
    ms(B("CT"), 0.0)
    for c in range(8):
        cp(B("CT", offs[c] + 16 * c, offs[c] + 16 * c + 16), S(MASK, 0, 16), "av"[c & 1], -0.5)
    ms(B("CT", 0, TRI, 144), 4096.0)
    ms(B("CT", 16, TRI, 160), 4096.0)
    DUMP = new("c32", 16)
    ts(DUMP, B("xi", 0, 16), -32.0, DC, AL.mult, AL.add)
    cp(nBlk, Blk16, "v", -1.0)
    cp(M1, Mh)
    B1, B2, Bn1 = times(S(Blk16, 0, 128, 16), 1.0), times(S(Blk16, 0, 128, 16), 2.0), S(nBlk, 0, 128, 16)
    nI, I16, If, I4, Kc = times(I, -1.0), times(I, 1.0, "ch"), times(I, 1.0, "c32"), times(I, 4096.0), times(xm, 0.0625)
    RST, SEG, RUN = new("c32"), new("ch"), new("cb")
    ts(RST, xm, 0.0, 1000000.0, AL.is_equal, AL.mult)
    M2, Mn = times(M1, 2.0), times(M1, -1.0)
    part = {}

    def nB(who):
        if who == "vvvv":
            return nBlk
        if who not in part:
            part[who] = times(nBlk, 1.0)
            for r in range(4):
                if who[r] == "a":
                    ms(S(part[who], r, 128, 4), 0.0)
        return part[who]
    for t in range(1, RO + 1):
        nB(C["D2"][t])
    ts(SEG, xm, 0.0, None, AL.not_equal)
    ts(RUN, xm, 0.0, None, AL.is_equal)
    THn, I24, In24 = times(xm, -85.0, "ch"), times(I, 2.0 ** 24), times(I, -2.0 ** 24)
    hI, I15, Ms = times(I, 0.5), times(I, -1.5), times(M1, 0.0625)
    K128, ONES, K120, THu, TriU, t2, t3 = new("cb"), new("cb"), new("cb", 32), new("ch"), new("cb"), new("c32"), new("c32")
    ms(K128, 1.0 / 128)
    ms(ONES, 1.0)
    ms(K120, -120.0 / 4096)
    ms(B("cum", HS, 2 * PW, PW), 1.0)
    ts(THu, ONES, THR, None, AL.mult)
    cp(t2, Blk16, "a", -2.0 ** 24)
    select(t3, t2, [[-1, 128]], AL.is_gt, 0.0, 1)
    select(TriU, t3, [[-1, 128]], AL.not_equal, 2.0 ** 24, 1)
    iota(B("TR"), [[1, XW + 8]], -8, 0)
    if "1" in C["tr3"]:
        iota(B("T3"), [[1, XW]], 0, 0)
    tsm([(col("ci", 4), col("ld_w", 0), 4080, None, AL.bitwise_and), (col("ci", 5), col("ld_w", 0), 15, None, AL.bitwise_and),
         (col("ci", 6), col("ld_w", 0), 127, None, AL.bitwise_and), (col("ci", 7), col("ld_w", 0), 2048, None, AL.bitwise_and)])
    cp(B("cf", 5, 9), B("ci", 4, 8))
    ts(WC, WC, -2.0, WH, AL.mult, AL.add)
    cWH, cWL, Mw = new("cb"), new("cb"), new("cb", 144)
    tsm([(cWH, nBlk, WC, -1.0 / 4096, AL.mult, AL.mult), (cWL, nBlk, WL, -1.0 / 4096, AL.mult, AL.mult), (Mw, M1, W7, None, AL.mult)])

    def M(m, d):
        return S(m, 15 - d, 143 - d)

    def wrap(out, m, src, block=False):
        n = cnt(out)
        return [(out, M(m, d), S(src, n * d, n * d + n) if block else S(src, d, None, 16)) for d in range(16)]

    def send(t):
        s = add("pool", ["send"], [], [B("snd", t * PW, t * PW + PW)], 1.0, t=t, sem="left", lat=1.0)
        out = B("rcv", t * PW, t * PW + PW) if t < 2 * RO else col("home", t - 2 * RO)
        return add("none", [], [out], [], MOVE, sem="arr%d" % t, after=[s], lat=0.0)

    def lists(k, src, rep, wr, out, shift, keep, plain=None):
        eq, sc, da, db = "eq%d" % k, B("sc%d" % k), B("da%d" % k), B("db%d" % k)
        mm([wrap(wr, Mh, src), [(rep, Blk16, src)]])
        if plain:
            cp(plain, wr)
        for part in ((0, 7, 1, 6), (2, 5, 3, 4)):
            tsm([(B(eq, offs[c], offs[c] + 16 * c + 16), S(rep, 0, 16 * c + 16), S(wr, c, c + 1), None, AL.not_equal) for c in part])
        cp(keep, rep, "a")
        scan(sc, B("CT"), B(eq), AL.add, AL.min)
        tt(da, IX(sc, B("eo", 0, 1)), DUMP, AL.mult)
        tt(db, S(da, 0, 8), wr, AL.max)
        ts(out, db, shift, None, AL.add)

    def vr(t):
        return B("vr", NU * t, NU * t + NU)

    def vw(t):
        return B("vw", 8 * t, 8 * t + 8)

    def vo(t):
        return B("vo", 8 * t, 8 * t + 8)

    def place_lists(t):
        lists(0, B("sel"), B("PN", 0, 128), B("PN", 128, 136), vo(t), 0.0, vr(t), vw(t))

    def rewrap(out, win, lst, m1, m2):
        tt(m1, IX(win, lst), MASK, AL.mult)
        scan(m2, SEG, m1, AL.mult, AL.max)
        cp(out, S(m2, 15, None, 16))

    def gather(dst, lst, n, who, s0=0):
        k = n // len(who)
        for q, e in enumerate(who):
            c = s0 + q * k
            cp(B(dst, 16 * c, 16 * (c + k)), IX(B("X", 0, NP), B(lst, c, c + k)), e)

    flip = [0]

    def dists(src, tmp, opnd, rep, who, nl, first, red, rest, s0=0):
        base, grp = 16 * s0, len(ops)
        mm(first, grp=grp, opens=True)

        def a(l):
            return B(src, base + l, base + 2048, 16)
        for r in range(4):
            ls, lo = [l for l in range(r, nl, 4)], base + 512 * r
            if who[r] == "v":
                mm(rest(r) + [red(l, "v", None, a(l))[1] for l in ls], grp=grp)
                for two in (ls[:2], ls[2:]):
                    tiles = [(l, B(tmp, lo + 128 * (l // 4), lo + 128 * (l // 4) + 128)) for l in two]
                    for l, tile in tiles:
                        tt(tile, a(l), rep, AL.max)
                    mm([red(l, "v", tile, None)[0] for l, tile in tiles], grp=grp)
            else:
                bank = "PD%d" % flip[0]
                flip[0] ^= 1
                mm([[(B(bank, 128 * q, 128 * q + 128), I, a(l)), (B(bank, 128 * q, 128 * q + 128), nI, opnd)] for q, l in enumerate(ls)])
                act(B(tmp, lo, lo + 128 * len(ls)), B(bank, 0, 128 * len(ls)), AF.Abs)
                mm([red(l, "a", B(tmp, lo + 128 * q, lo + 128 * q + 128), None)[0] for q, l in enumerate(ls)], grp=grp)

    cp(B("sel"), B("ld_v"))
    place_lists(0)

    def aold(t):
        return B("A", NU * (1 - (t & 1)), NU * (1 - (t & 1)) + NU)
    cp(B("A16"), B("ld_a"))
    cp(aold(1), B("ld_a"), "v", 4096.0)
    cp(B("jh"), B("ld_j"))
    mm(wrap(B("PS0", 0, 16), Mh, B("jh")))
    for hf in range(2):
        cp(B("snd", hf * PW + HS, hf * PW + PW), B("PS0", 8 * hf, 8 * hf + 8))
        send(hf)
    for o in ops:
        o["boost"] = C["early"][1] if o["on"] in ("sync", "none") or "sem" in o else C["early"][0]

    def users_a(t):
        cp(B("n16"), IX(B("NB"), vw(t - 1)))
        cp(B("nh"), B("n16"))
        k = len(ops)
        gather("g2", "A16", NU, C["G2"][t])
        for o in ops[k:]:
            o["boost"] = C["early"][2] if t == 1 else C["walk"][0]
        k = len(ops)
        gather("g1", "n16", NU, C["G1"][t])
        for o in ops[k:]:
            o["boost"] = C["walk"][1] if t > 1 else 0.0
        key = B("PK", 0, 128)

        def red1(k, path, tile, a):
            o = B("PK", k, 128, 16)
            return [(o, tile, B1)] if path == "a" else [(o, tile, B2), (o, a, Bn1)]
        if "v" in C["D1"][t]:
            mm([(B("PO", 256, 384), I, B("Y"))])
        dists("g1", "e1", B("Y"), B("PO", 256, 384), C["D1"][t], 16, [(key, I, Kc)], red1,
              lambda r: [(B("PK", r, 128, 4), B("Y"), S(nBlk, r, 128, 4))])
        scan(B("pm"), RST, key, AL.add, AL.min)
        add("dve", [lambda g, T: g.vector.tensor_tensor_scan(T.df[:, ::-1], ap(T, RST), T.pm[:, ::-1], 0.0, AL.add, AL.min)],
            [B("df")], [RST, B("pm")], [("v", 128)])
        tt(B("eqT"), key, B("df"), AL.is_equal)
        mm([(B("PK", 128, 256), B("eqT"), I4), (B("PK", 128, 256), I16, B("nh"))])
        act(B("sel"), B("PK", 128, 256), AF.Relu, bias=-4096.0)
        place_lists(t)
        cp(B("xn"), IX(B("X", 0, NP), vw(t)), C["xn"][t])
        who = C["D2"][t]

        def red2(l, path, tile, a):
            o = B("PU", 0, 128)
            return [(o, M(M1, l), tile)] if path == "a" else [(o, M(M2, l), tile), (o, M(Mn, l), a)]
        if "v" in who:
            mm([(B("PO", 384, 512), I, B("xn"))])
        dists("g2", "e2", B("xn"), B("PO", 384, 512), who, 16, [(B("PU", 0, 128), I16, THu)], red2,
              lambda r: [(B("PU", 0, 128), nB(who), B("xn"))] if r == who.index("v") else [])
        mm([[(B("PK", 0, 128), I, B("xn")), (B("PK", 0, 128), I, B("Y"))], [(B("PK", 128, 256), I, B("xn")), (B("PK", 128, 256), nI, B("Y"))]])
        ts(B("xw"), B("PK", 0, 128), 0.5, -0.25, AL.mult, AL.add)
        act(B("Y"), B("PK", 128, 256), AF.Abs)
        mm([(B("PK", 256, 384), If, aold(t)), (B("PK", 256, 384), nBlk4, B("sel"))])

    def users_b(t):
        TRW = B("TR", 8, 8 + NP)
        if t == 1:
            ts(B("nw"), B("PU", 0, 128), -120.0, None, AL.is_gt)
        else:
            ts(B("nw"), B("PU", 0, 128), col("fa", 1), col("fa", 0), AL.add, AL.is_gt)
        tt(B("dA"), B("nw"), B("PK", 256, 384), AL.mult)
        tt(aold(t + 1), aold(t), B("dA"), AL.subtract)
        cp(IX(B("X"), vo(t)), B("xw"))
        cp(B("XV"), IX(B("X", 0, NP), vw(t)), C["xv"][t])
        if t > 1:
            mm([(B("PU", 128, 256), If, aold(t)), (B("PU", 128, 256), TriU, B("nw"))])
            if C["sb"][t] == "a":
                act(B("sb"), B("PU", 128, 256), AF.Relu, bias=-4095.0, scale=1.0 / 4096)
            else:
                ts(B("PU", 128, 256), B("PU", 128, 256), 1.0 / 4096, -4095.0, AL.mult, AL.add)
                ts(B("sb"), B("PU", 128, 256), 0.0, None, AL.max)
            lists(1, B("sb"), B("PU", 256, 384), B("PU", 384, 392), B("bo", 0, 8), 7.0, B("br", 0, NU))
            ts(IX(B("TR"), B("bo", 0, 8)), B("br", 0, NU), 1.0, -1.0, AL.mult, AL.add)
        cp(IX(B("TR", 8), vo(t - 1)), vr(t))
        if C["tr3"][t - 1] == "1":
            for k in range(t):
                m1, m2, br = (B(n, NU * k, NU * k + NU) for n in ("t1", "t2", "br"))
                l1, l2 = B("bo", 8 + 16 * k, 16 + 16 * k), B("bo", 16 + 16 * k, 24 + 16 * k)
                if k == t - 1:
                    l1 = vw(t)
                else:
                    rewrap(l1, TRW, vw(k), m1, m2)
                rewrap(l2, TRW, l1, m1, m2)
                cp(br, IX(TRW, l2), "a")
                cp(IX(B("T3"), vo(k)), br)
        if t < RO:
            cp(B("A16"), aold(t + 1), "v", 1.0 / 4096)
        else:
            cp(B("df"), aold(RO + 1), "a", 1.0 / 4096)
            dma("sync", "s_yv", lambda g, T: g.sync.dma_start(T.yv[:], T.vr[0:128:16, NU * RO:NU * RO + NU]), [], [vr(RO)], 2.0)
            dma("sync", "s_ya", lambda g, T: g.sync.dma_start(T.ya[:], T.df[:]), [], [B("df")], 2.0)
            dma("sync", "s_yy", lambda g, T: g.sync.dma_start(T.yy[:], T.Y[:]), [], [B("Y")], 2.0)
            dma("sync", "s_yt", lambda g, T: g.sync.dma_start(T.yt[:], T.TR[0:128:16, 8:8 + NP]), [], [B("TR")], 2.5)

    def seekers(t, hf):
        lo, hi, c8 = HS * hf, HS * hf + HS, 8 * hf
        r0, s0 = (2 * t - 2 + hf) * PW, (2 * t + hf) * PW
        z, jw = B("rcv", r0, r0 + HS), B("rcv", r0 + HS, r0 + PW)
        last, bank = t == RO, "PS%d" % hf
        TRW, XS = B("TR", 8, 8 + NP), B("X", 0, NP)

        def H(name):
            return B(name, lo, hi)

        def P(name):
            return B(name, PW * hf, PW * hf + PW)

        def W(name):
            return B(name, c8, c8 + 8)
        j16, pz = W("j16"), B("PO", lo, hi)
        p0, p1, p2, p3 = B(bank, 0, HS), B(bank, HS, 2 * HS), B(bank, 2 * HS, 3 * HS), B(bank, 3 * HS, 4 * HS)
        cp(j16, jw)
        mm([(p0, I, K128), (p0, cWH, z), (p0, cWL, z)])
        ts(H("q"), p0, -2079.5 / 4096, None, AL.add)
        tt(p1, H("q"), p0, AL.subtract)
        if C["Bh"][t][hf] == "e":
            cp(H("Aj"), IX(aold(t), j16), "a")
            tt(H("Bh"), IX(B("dA"), j16), H("Aj"), AL.subtract)
        else:
            cp(H("Bh"), IX(aold(t + 1), j16), C["Bh"][t][hf], -1.0)
        tt(H("u2"), H("Bh"), p1, AL.mult)
        ts(H("u1"), H("u2"), 5, 2047, AL.arith_shift_right, AL.bitwise_and)
        cp(H("h16"), H("u1"))
        gather("g3", "h16", HS, C["G3"][t][4 * hf:4 * hf + 4], lo)
        cp(H("vj"), IX(vr(t), j16), C["vj"][t][hf])
        mm([(pz, I, z)])
        cp(H("xj"), IX(B("XV"), j16), C["xj"][t][hf])
        mm([(p0, hI, H("xj")), (p0, I15, z)])
        ts(H("q"), p0, 0.25, None, AL.add)
        mm(wrap(S(p3, 0, 8), Mw, z, last))
        cp(W("w1"), S(p3, 0, 8))
        ts(W("w2"), W("w1"), 127, None, AL.bitwise_and)
        if last:
            cp(H("jr"), IX(B("xi", 0, 128), j16), "a")
            mm(wrap(S(p3, 8, 16), Ms, H("jr"), True))
            cp(W("jb"), S(p3, 8, 16))
            jw = W("jb")
        tt(W("dw"), W("w2"), jw, AL.subtract)

        def red(l, path, tile, a):
            o = S(p2, l + 1, HS, 16)
            return [(o, tile, B1)] if path == "a" else [(o, tile, B2), (o, a, Bn1)]
        dists("g3", "e3", z, pz, C["D3"][t][4 * hf:4 * hf + 4], 15, [(p2, I16, THn)], red,
              lambda r: [(S(p2, (r + 1) % 4, HS, 4), z, S(nBlk, (r + 1) % 4, 128, 4))], lo)
        cum = P("cum")
        grp = len(ops)
        mm([(p1, If, H("Bh"))], grp=grp, opens=True)
        scan(S(cum, 0, HS), p2, RUN, AL.min, AL.max)
        mm([(p1, S(cum, 0, HS), In24), (p1, S(cum, 1, HS + 1), I24)], grp=grp)
        act(H("ss"), p1, AF.Relu, bias=BIAS, scale=-1.0 / 4096)
        mm(wrap(S(p3, 16, 24), Mh, H("ss")))
        c0 = 0
        if C["tr3"][t - 1] == "1":
            c0, TRW = 2, B("T3", 0, NP)

        def pw(c):
            return B("pw", 32 * hf + 8 * c, 32 * hf + 8 * c + 8)
        cp(pw(c0), S(p3, 16, 24))
        fd = H("fd")
        for c in range(c0, 3):
            if c == 2:
                tt(fd, IX(TRW, pw(c)), H("vj"), AL.is_equal)
            rewrap(pw(c + 1), TRW, pw(c), H("m1"), H("m2"))
        if not last:
            o = B("PN", 400 + 32 * hf, 432 + 32 * hf)
            mm([(o, ONES, S(fd, 32 * q, 32 * q + 32)) for q in range(4)] + ([] if hf else [(o, ONES, K120)]))
        tt(H("fe"), fd, H("q"), AL.mult)
        tt(H("zz"), H("fe"), pz, AL.add)
        tt(H("tz"), IX(XS, pw(3)), H("zz"), AL.subtract)
        act(B("snd", s0, s0 + HS), H("tz"), AF.Abs)
        mm(wrap(S(p3, 24, 32), Ms, fd, last))
        tt(W("tw"), S(p3, 24, 32), W("dw"), AL.mult)
        tt(B("snd", s0 + HS, s0 + PW), W("tw"), jw, AL.add)
        send(2 * t + hf)

    def finds():
        add("dve", [lambda g, T: g.vector.tensor_reduce(T.fa[:, 0:1], T.PN[:, 400:464], AxisListType.X, AL.add)],
            [col("fa", 0)], [B("PN", 400, 464)], [("v", 64)])
        ts(col("fa", 1), col("fa", 0), 1.5 * 2.0 ** 31, 1.5 * 2.0 ** 31, AL.add, AL.subtract)

    users_a(1)
    users_b(1)
    for t in range(1, RO + 1):
        seekers(t, 0)
        seekers(t, 1)
        if t < RO:
            finds()
            users_a(t + 1)
            users_b(t + 1)

    def store(hf):
        lo = HS * hf
        dma("sync", "s_yz%d" % hf, lambda g, T: g.sync.dma_start(T.yz[:, lo:lo + HS], T.home[hf, :, 0:HS]), [], [col("home", hf)], 2.0)
        dma("pool", "s_yj%d" % hf, lambda g, T: g.dma_start(T.yj[:, lo:lo + HS], T.home[hf, :, HS:PW]), [], [col("home", hf)], 2.5)
    store(0)
    store(1)
    return ops


def unordered(ops, d, i):
    e = ops[i]["on"]
    return e == ops[d]["on"] and (e == "pe" or (CFG["free"] and e in ("dve", "act") and d not in ops[i]["raw"] and "sem" not in ops[d]))


def schedule(ops):
    n = len(ops)
    pred = [sorted(set(o["deps"]) | set(o.get("soft", []))) for o in ops]
    eng = [o["on"] for o in ops]
    cost = [o["cost"] for o in ops]
    lat = [o.get("lat", 0.0) for o in ops]
    succ = [[] for _ in ops]
    gap = {}
    for i, o in enumerate(ops):
        for d in pred[i]:
            if d not in o["deps"]:
                gap[d, i] = -lat[d]
            else:
                gap[d, i] = 0.0 if unordered(ops, d, i) else (LAT0 if eng[d] == eng[i] else LAT1)
            succ[d].append((i, gap[d, i]))

    def sweep(prio):
        left = [len(b) for b in pred]
        can = [0.0] * n
        ready = [i for i in range(n) if left[i] == 0]
        busy, done, at = {}, [0.0] * n, [0.0] * n
        while ready:
            i = max(ready, key=lambda x: prio[x])
            e, st = eng[i], can[i]
            held = [x for x in busy.get(e, []) if x[1] > st]
            for b in ops[i]["banks"]:
                held += [(x[0] - LAT1, x[1] + LAT1) for x in busy.get(b, []) if x[2] != e and x[1] + LAT1 > st]
            for x in sorted(held):
                if x[0] >= st + cost[i] - 1e-9:
                    break
                st = max(st, x[1])
            at[i] = st
            done[i] = st + cost[i] + lat[i]
            if e != "none":
                busy.setdefault(e, []).append((st, st + cost[i]))
            for b in ops[i]["banks"]:
                busy.setdefault(b, []).append((st, st + cost[i], e))
            ready.remove(i)
            for s, w in succ[i]:
                can[s] = max(can[s], done[i] + w)
                left[s] -= 1
                if left[s] == 0:
                    ready.append(s)
        order = sorted(range(n), key=lambda x: (at[x], x))
        bank, extra = {}, []
        for i in order:
            for b in ops[i]["banks"]:
                if b in bank and eng[bank[b]] != eng[i]:
                    extra.append((i, bank[b]))
                bank[b] = i
        return max(done), order, at, extra, done

    prio = [0.0] * n
    for i in reversed(range(n)):
        prio[i] = cost[i] + lat[i] + max([prio[s] + w for s, w in succ[i]] + [0.0])
    rng = np.random.default_rng(CFG["seed"])
    prio = [p + o.get("boost", 0.0) for p, o in zip(prio, ops)]
    for i in reversed(range(n)):
        prio[i] = max([prio[i]] + [prio[s] + 0.01 for s, w in succ[i]])
    best = now = sweep(prio)
    turns = CFG["turns"]
    for turn in range(turns):
        _, order, at, extra, done = now
        last, prev = {}, {}
        for i in order:
            prev[i] = last.get(eng[i]) if eng[i] != "none" else None
            last[eng[i]] = i
        held = dict(extra)
        i, jams = max(range(n), key=lambda x: done[x]), []
        while True:
            d = max(pred[i], key=lambda x: done[x] + gap[x, i]) if pred[i] else None
            t = done[d] + gap[d, i] if d is not None else 0.0
            if t < at[i] - 1e-6:
                j = prev[i]
                if i in held and (j is None or done[held[i]] + LAT1 > at[j] + cost[j]):
                    j = held[i]
                if j is not None:
                    jams.append((i, j))
                    d = j
            if d is None:
                break
            i = d
        p2 = list(prio)
        for _ in range(1 + int(rng.integers(0, 2))):
            i, j = jams[int(rng.integers(0, len(jams)))]
            if rng.random() < 0.5:
                p2[j] = min(p2[j], p2[i]) - float(rng.uniform(0.0, 3.0))
            else:
                top, todo = max(p2[i], p2[j]) + float(rng.uniform(0.0, 1.0)), [i]
                while todo:
                    x = todo.pop()
                    if p2[x] < top:
                        p2[x] = top
                        todo.extend(pred[x])
        new = sweep(p2)
        if new[0] <= now[0] + CFG["tilt"] * (1.0 - turn / turns) * float(rng.random()):
            now, prio = new, p2
            if new[0] < best[0]:
                best = new
    for i, o in enumerate(ops):
        o["at"] = best[2][i]
    for i, d in best[3]:
        ops[i]["deps"].add(d)
    return best[1], best[0]


PLAN = {}


def plan():
    if not PLAN:
        PLAN["ops"] = build()
        PLAN["order"], PLAN["span"] = schedule(PLAN["ops"])
        sums = {}
        for i in PLAN["order"]:
            o = PLAN["ops"][i]
            if o.get("grp") is not None:
                sums.setdefault(o["grp"], []).append(o)
        for part in sums.values():
            part[0]["calls"][0][3] = True
            part[-1]["calls"][-1][4] = True
    return PLAN["ops"], PLAN["order"]


def target(T, r, t):
    n = len(T.cores)
    return T.cores[(r + 1) % n] if t < 2 * RO else T.cores[(r - RO) % n]


def relay(T, topo, r):
    c = T.cores[r]
    ok = [h for h in topo.cores_of(c) if h not in T.cores and all(topo.may_write(h, target(T, r, t)) for t in range(MOVES))]
    return sorted(ok, key=lambda h: topo.die(h) != topo.die(c))[0]


def width(mask):
    return bin(mask).count("1")


def rank_program(g, core, T, topo):
    rank = T.rank_of(core)
    n = len(T.cores)
    ops, order = plan()
    if rank is None:
        for r in range(n):
            if relay(T, topo, r) == core:
                total = 0
                for t in [ops[i]["t"] for i in order if "t" in ops[i]]:
                    d = target(T, r, t)
                    rid, pid = topo.addr(d, core)
                    g.wait_ge(T.sem["rel%d" % t], width(topo.mask(T.cores[r], core)))
                    out = T.rcv[:, t * PW:t * PW + PW] if t < 2 * RO else T.home[t - 2 * RO]
                    g.remote_dma(out, T.hop[t], T.sem["arr%d" % t], T.sem.left, pid, rid, topo.mask(core, d))
                    total += width(topo.mask(core, d))
                g.wait_ge(T.sem.left, total)
        return
    h = relay(T, topo, rank)
    queue = {"dve": g.vector, "act": g.scalar, "pe": g.tensor, "pool": g, "sync": g.sync}
    count = {}
    known = dict((q, {}) for q in queue)
    token, clock = {}, {}
    for i in order:
        o = ops[i]
        e = o["on"]
        if e == "none":
            t = int(o["sem"][3:])
            src = (rank - 1) % n if t < 2 * RO else (rank + RO) % n
            token[i] = (o["sem"], width(topo.mask(relay(T, topo, src), core)))
            clock[i] = {token[i][0]: token[i][1]}
            continue
        need = {}
        for d in o["deps"]:
            if unordered(ops, d, i):
                continue
            s, c = token[d]
            if c > need.get(s, (0, 0))[0]:
                need[s] = (c, d)
        for s, (c, d) in sorted(need.items(), key=lambda x: -x[1][1]):
            if known[e].get(s, 0) < c:
                queue[e].wait_ge(T.sem[s], c)
                for s2, c2 in clock[d].items():
                    known[e][s2] = max(known[e].get(s2, 0), c2)
        ins = o["ins"][e]
        if ins == ["send"]:
            t = o["t"]
            rid, pid = topo.addr(h, core)
            m = topo.mask(core, h)
            g.remote_dma(T.hop[t], T.snd[:, t * PW:t * PW + PW], T.sem["rel%d" % t], T.sem.left, pid, rid, m)
            count["left"] = count.get("left", 0) + width(m)
            token[i] = ("left", count["left"])
        elif "sem" in o:
            ins[0](g, T).then_inc(T.sem[o["sem"]], 16)
            token[i] = (o["sem"], 16)
            count[o["sem"]] = 16
        else:
            for q, f in enumerate(ins):
                x = f(g, T)
                if e != "pe" or q == len(ins) - 1:
                    x.then_inc(T.sem[e], 1)
                    count[e] = count.get(e, 0) + 1
            token[i] = (e, count[e])
        clock[i] = dict(known[e])
        clock[i][token[i][0]] = token[i][1]
    for s, c in sorted(count.items()):
        if known["pool"].get(s, 0) < c:
            (g.sync if s in ("s_yv", "s_ya", "s_yy", "s_yt", "s_yz0", "s_yz1") else g).wait_ge(T.sem[s], c)
